import numpy as np, ml_dtypes
CORES = [2,6,10,14,18,22,26,30]
N = 8
BF = ml_dtypes.bfloat16
W, E, B, C, RO, NC = 2048, 1024, 128, 10, 3, 32
def group(rng, noise, good, mode, proto):
    n = W // NC; mem = rng.permutation(W).reshape(NC, n); cl = np.zeros(W, np.int64); cl[mem] = np.arange(NC)[:, None]
    x = np.minimum(np.maximum(proto[:, cl] + rng.integers(-noise, noise + 1, (16, W)), 0), 63)
    nx = rng.integers(0, NC, (16, NC))
    if mode == 1: nx[:] = np.arange(NC)
    if mode == 2: nx[:] = cl[0]
    if mode == 3: nx[:] = cl[W - 1]
    l = mem[nx[:, cl], rng.integers(0, n, (16, W))]
    if mode == 1: l[:] = np.arange(W)
    if mode == 2: l[:] = 0
    if mode == 3: l[:] = W - 1
    i = np.zeros((16, E), np.int64); q = rng.integers(0, NC, E)
    for k in range(16):
        i[k] = mem[q, rng.integers(0, n, E)]
        if k < 15:
            go = nx[k, q]; q = np.where(good[k], go, (go + rng.integers(1, NC, E)) % NC)
    return x, i, l
def parts(rng, style):
    x = np.zeros((N, 8, 16, W), np.int64); i = np.zeros((N, 8, 16, E), np.int64); l = np.zeros((N, 8, 16, W), np.int64)
    for a in range(N):
        for g in range(8):
            noise = int(rng.integers(1, 4)); mode = 0; proto = rng.integers(0, 64, (16, NC))
            good = rng.random((15, E)) < rng.choice(np.array([0.2, 0.6, 0.8, 0.95, 1.0]), E)
            if style == "ties": noise = 0; proto = 16 + 8 * rng.integers(0, 2, (16, NC))
            if style == "corners":
                noise = 0; mode = (a + g) % 4; n = rng.choice(np.array([0, 1, C - 1, C, C + 1, 15]), E)
                good = np.argsort(np.argsort(rng.random((15, E)), axis=0), axis=0) < n
            x[a, g], i[a, g], l[a, g] = group(rng, noise, good, mode, proto)
    t = np.stack([rng.integers(20, 70, (N, 8, 16)), rng.integers(200, 420, (N, 8, 16))], axis=-1)
    return x, rng.integers(0, 64, (N, 8, 16, E)), i, l, rng.integers(0, 64, (N, 8, 16, B)), rng.integers(0, 256, (N, 8, 16, 1)), rng.integers(0, 2048, (N, 8, 16, 2)), t
def pack(x, gs, i, l, z, w, h, t):
    def bf(v): return np.ascontiguousarray(v.reshape(N, 128, -1)).astype(np.float32).astype(BF)
    def whole(v): return np.ascontiguousarray(v.reshape(N, 128, -1)).astype(np.int32)
    return {"xc": bf(x), "gi": bf(gs), "ix": whole(i), "lk": whole(l), "zc": bf(z), "wt": whole(w), "hk": whole(h), "th": whole(t)}
def ends(rng, lo, hi, shape, share):
    v = np.where(rng.random(shape) < 0.5, lo, hi)
    return np.where(rng.random(shape) < share, v, rng.integers(lo, hi + 1, shape))
def records(rng, n):
    k = rng.integers(0, 3, (N, 8, 1, n))
    return np.where(k == 0, 0, np.where(k == 1, 63, ends(rng, 0, 63, (N, 8, 16, n), 1.0)))
def full(rng, p):
    u = rng.permutation(4096); f, k = np.unique(((u * u >> 5) + p * u) & (E - 1), return_index=True)
    return u[rng.permutation(k)[:B]]
def setup_inputs(rng):
    return pack(*parts(rng, "plain"))
def setup_inputs_ties(rng):
    x, gs, i, l, z, w, h, t = parts(rng, "ties")
    gs = 16 + 8 * rng.integers(0, 2, gs.shape); z = 16 + 8 * rng.integers(0, 2, z.shape)
    t = rng.choice(np.array([56, 63, 64, 65, 72]), t.shape)
    for a in range(N):
        for g in (6, 7):
            v = (256, 257, 259, 513, 515, 767, 1005, 1007)[(a + g) & 7]; base = int(rng.integers(0, 1008 - v))
            m = rng.permutation(W); low = np.flatnonzero(m < W // 2); high = np.flatnonzero(m >= W // 2)
            size = base + np.where(m < W // 2, 0, v + (rng.random(W) < 0.3).astype(np.int64))
            x[a, g] = (size >> 4) + (np.arange(16)[:, None] < (size & 15)).astype(np.int64)
            i[a, g] = low[rng.integers(0, W // 2, (16, E))]; l[a, g] = high[rng.integers(0, W // 2, (16, W))]
            t[a, g, :, 0] = v; t[a, g, :, 1] = 1008
    return pack(x, gs, i, l, z, w, h, t)
def setup_inputs_corners(rng):
    x, gs, i, l, z, w, h, t = parts(rng, "corners")
    for a in range(N):
        for g in range(8):
            kind = (3 * a + g) % 4
            if kind == 0: w[a, g] = 255
            if kind == 1: w[a, g] = 255 * rng.integers(0, 2, (16, 1))
            if kind == 2: w[a, g] = 0; w[a, g, 15] = 1
            t[a, g, :, 0] = (0, 1, 40, 0, 0, 1008, 40, 1)[(a + g) % 8]
            t[a, g, :, 1] = rng.choice(np.array([0, 340, 1008]), 16)
            h[a, g] = np.where(rng.random((16, 2)) < 0.4, 2047 * rng.integers(0, 2, (16, 2)), h[a, g])
    k = rng.integers(0, 4, (N, 8, 1, B)); z = np.where(k == 0, 0, np.where(k == 1, 63, z))
    k = rng.integers(0, 4, (N, 8, 1, E)); gs = np.where(k == 0, 0, np.where(k == 1, 63, gs))
    i = np.where(rng.random((N, 8, 1, E)) < 0.1, (W - 1) * rng.integers(0, 2, (N, 8, 1, E)), i)
    return pack(x, gs, i, l, z, w, h, t)
def setup_inputs_crowd(rng):
    x, gs, i, l, z, w, h, t = parts(rng, "plain")
    w[:, 0::4] = 0; w[:, 0::4, 5] = 1; z[:, 0::4, 5] = rng.integers(0, 6, (N, 2, B)); h[:, 0::4, :, 0] = 0
    i[:, 1] = rng.choice(np.array([0, 1, W // 2, W - 2, W - 1]), (N, 16, E)); gs[:, 1] = 30
    w[:, 2] = 0
    z[:, 3] = z[:, 3][..., rng.integers(0, 3, B)]
    for a in range(N):
        for g in (5, 6, 7):
            w[a, g] = 0; w[a, g, 0] = 1; w[a, g, 1] = 64; gs[a, g] = 0
            p = int(h[a, g, 0, 0]); u = full(rng, p)
            if g == 5: u[B // 2:] = u[:B // 2]
            z[a, g, 0] = u & 63; z[a, g, 1] = u >> 6
            e = ((u * u >> 5) + p * u) & (E - 1)
            if g == 5:
                side = rng.random(B // 2) < 0.5; side[0] = True; side[1] = False; near = np.concatenate([side, ~side])
                x[a, g] = rng.integers(16, 25, (16, W)); i[a, g] = rng.integers(0, W, (16, E))
                z[a, g, 2:] = np.where(near, rng.integers(16, 25, (14, B)), rng.integers(56, 64, (14, B)))
                t[a, g, :, 0] = 0; t[a, g, :, 1] = rng.integers(206, 448, 16)
            if g == 6:
                o = rng.permutation(W); i[a, g][:, e] = o[(np.arange(16)[:, None] % (W // B)) * B + np.arange(B)]
                t[a, g, :, 0] = 0
            if g == 7: t[a, g, :, 0] = 1008
    t[2, :, :, 0] = 0
    gs[2, 3] = 30; c = int(rng.integers(0, W)); u = np.add.reduce(w[2, 3] * z[2, 3], axis=0) & 4095
    e = ((u * u >> 5) + h[2, 3, 0, 0] * u) & (E - 1)
    i[2, 3][:, e] = c; l[2, 3][:, c] = c
    return pack(x, gs, i, l, z, w, h, t)
def setup_inputs_spread(rng):
    x, gs, i, l, z, w, h, t = parts(rng, "plain")
    x = x >> rng.integers(0, 7, (N, 8, 1, W)); gs = gs >> rng.integers(0, 7, (N, 8, 1, E)); z = z >> rng.integers(0, 7, (N, 8, 1, B))
    i[:, ::2] = (W * rng.random((N, 4, 16, E)) ** 3).astype(np.int64); l[:, ::4] = (W * rng.random((N, 2, 16, W)) ** 3).astype(np.int64)
    w = np.exp2(8 * rng.random(w.shape)).astype(np.int64); h = np.exp2(11 * rng.random(h.shape)).astype(np.int64)
    t = np.minimum(np.exp2(10.2 * rng.random(t.shape)).astype(np.int64), 1008)
    return pack(x, gs, i, l, z, np.minimum(w, 255), np.minimum(h, 2047), t)
def setup_inputs_ends(rng):
    x = records(rng, W); gs = records(rng, E); z = records(rng, B)
    x[:, 0::2, :, 0] = 63; x[:, 0::2, :, W - 1] = 0; x[:, 1::2, :, 0] = 0; x[:, 1::2, :, W - 1] = 63
    i = ends(rng, 0, W - 1, (N, 8, 16, E), 0.75); l = ends(rng, 0, W - 1, (N, 8, 16, W), 0.75)
    w = ends(rng, 0, 255, (N, 8, 16, 1), 0.75); w[:, 7] = 255
    h = ends(rng, 0, 2047, (N, 8, 16, 2), 0.8); t = ends(rng, 0, 1008, (N, 8, 16, 2), 1.0)
    t[0, :, :, 0] = 1008; a = N - 1; t[a, 7, :, 0] = 0
    i[0, 5] = W - 1; l[0, 5, :, W - 1] = 0
    t[1, :, :, 0] = 1008; t[1, 6, :, 0] = 0
    w[1, 6] = 0; w[1, 6, 15] = 255; z[1, 6, 15] = 0; z[1, 6, 15, B - 1] = 63; h[1, 6, :, 0] = 2047 * rng.integers(0, 2, 16)
    i[1, 6] = W - 1; i[1, 6, :, 0] = 0; l[1, 6, :, 0] = 0; l[1, 6, :, W - 1] = 0
    v = z[a, 7]; v[:, B - 1] = 63; v[:, B - 2] = 0; v[15, B - 2] = 63; v[:, B - 3] = 0; v[:4, B - 3] = 63; v[4, B - 3] = 5
    h[a, 7, 0, 0] = 2047; h[a, 7, 1, 0] = 0; h[a, 7, 15, 1] = 2047
    h[a, 7, 15, 0] = ((E - 1 - (3777 * 3777 >> 5)) * pow(3777, -1, E)) % E
    c = ((3088 * 3088 >> 5) + h[a, 7, :, 0] * 3088) & (E - 1)
    gs[a, 7][:, c] = 0; gs[a, 7, :, E - 1] = v[:, B - 2]
    i[a, 7, :, c[1]] = 0; i[a, 7, :, c[0]] = W - 1; i[a, 7, :8, E - 1] = 0; i[a, 7, 8:, E - 1] = W - 1
    l[a, 7, :, 0] = 0; l[a, 7, :, W - 1] = 0
    return pack(x, gs, i, l, z, w, h, t)
def check_inputs(d):
    bad = []
    for k, lo, hi in (("xc", 0, 63), ("gi", 0, 63), ("ix", 0, W - 1), ("lk", 0, W - 1), ("zc", 0, 63), ("wt", 0, 255), ("hk", 0, 2047), ("th", 0, 1008)):
        v = np.asarray(d[k]).astype(np.float64)
        if not np.all((v >= lo) & (v <= hi) & (v == np.floor(v))): bad.append("range of " + k)
    return bad
def reference(xc, gi, ix, lk, zc, wt, hk, th):
    def cut(v): return np.asarray(v).astype(np.float32).astype(np.int64).reshape(N, 8, 16, -1)
    X, G, I, L, Z, w, h, t = cut(xc), cut(gi), cut(ix), cut(lk), cut(zc), cut(wt), cut(hk), cut(th)
    A = np.zeros(N, np.int64); lane = np.arange(B)
    for rnd in range(RO):
        count = np.zeros(N, np.int64)
        for a in range(N):
            r = (a - rnd) % N
            for g in range(8):
                z = Z[r, g]
                u = np.add.reduce(w[a, g] * z, axis=0) & 4095
                em = ((u * u >> 5) + h[a, g, :, 0:1] * u + A[a]) & (E - 1)
                d = np.add.reduce(np.abs(G[a, g][:, em] - z[:, None, :]), axis=0)
                e = em[np.argmin(d, axis=0), lane]
                J = I[a, g][:, e]
                x = X[a, g][:, J]
                y = X[a, g][:, np.take_along_axis(L[a, g], J, 1)]
                s = np.add.reduce(np.abs(y[:, :15] - x[:, 1:]), axis=0)
                far = np.add.reduce(np.abs(x - z[:, None, :]), axis=0)
                rec = np.add.reduce((s <= t[a, g, :15, 0:1]).astype(np.int64), axis=0) >= C
                fresh = ((u * u >> 4) + h[a, g, :, 1:2] * u) & (W - 1)
                col = np.where(rec[None, :] | (far > t[a, g, :, 1:2]), fresh, J)
                ks = np.argmax(s, axis=0)
                f, first = np.unique(e, return_index=True)
                I[a, g][:, f] = col[:, first]
                if rnd < RO - 1:
                    o = first[rec[first]]; G[a, g][:, e[o]] = z[:, o]
                q = np.flatnonzero(~rec); c, one = np.unique(J[ks[q], q], return_index=True); q = q[one]
                L[a, g][ks[q], c] = J[ks[q] + 1, q]
                count[a] += np.count_nonzero(rec)
                Z[r, g] = (z + np.maximum.reduce(x, axis=1)) >> 1
        A = count
    return {"yz": Z.reshape(N, 128, B).astype(np.float32).astype(BF), "yi": I.reshape(N, 128, E).astype(np.float32), "yl": L.reshape(N, 128, W).astype(np.float32)}

@@ -1,0 +1,590 @@
+from concourse.mybir import AluOpType, ActivationFunctionType
+
+ALU = AluOpType
+ACT = ActivationFunctionType
+RO = 3
+SEG = [8 * c * (c + 1) for c in range(9)]
+PSUM = ("p0", "p1", "p2", "p3", "p4", "p5", "p6", "p7")
+SCRATCH = {b: ("psum", [128, 512], "float32") for b in PSUM}
+for _t, _names in {
+    "float32": "IX:1152 LK:2192 ONES:128 IDF:128 BOF:128 SHF:128 HALF:128 RQ:128 M16:128 RMIN:128 RMAX:128 UT:128 MKEY:128 JJ0:128 JJ1:128 ACC:1 WLF:64 SG:128 HV:128 "
+               "NT:128 REP2:128 NOH:128 JN:128 TOLD:128",
+    "bfloat16": "XC:2048 GI:1152 Z0:128 Z1:128 Z2:128 ZR:128 ZN0:128 ZN1:128 ZN2:128 ZH:128 ZS:2048 ZREP:2048 ZT0:128 ZT1:128 RM:2048 ONESB:512 IDB:128 NIDB:128 HID:128 NHID:128 IDK:128 "
+                "NID4K:128 BOB:128 SHB:128 EB:432 G8:64 MROW:128 M24:128 M16B:128 MNEG:128 SEL:2048 RX:2048 RD:576 R1:576 R2:576 R3:576 WB:128 "
+                "DG:2048 AG:2048 DY:2048 AY:2048 GR:1024 XG:2064 XM:2048 CMP:128 RECS:128 RBS:128 XA:576 XS:576 AF:2048 NOHB:128",
+    "float16": "PD:128 QD:128 PW:128 QW:128 VH:128 ERM:128 ERU:128 ERM2:128 ERU2:128 JH:128 LG:2048",
+    "int32": "IXI:1024 LKI:2048 WTI:1 HKI:2 THI:2 PIO:16 PR:16 CIO:8 PWI:128 QWI:128 UI:128 UU:128 S5:128 BS:128 VQ:128 EI:128 EM:128 KMIN:128 KA:8 KMX:128 KJ:24",
+    "uint16": "OFFG:8 ENDS:2 EU:128 E8U:8 JU:128 NU:128 GOFF:8 NOFF:8 LOFF:8 JX8:8",
+}.items():
+    for _n in _names.split():
+        SCRATCH[_n.split(":")[0]] = ("sbuf", [128, int(_n.split(":")[1])], _t)
+PART = {}
+_at = 0
+for _n in "RF:1 WC:1 HKF:2 ACOL:1 BCOL:1 THF:2 JJC:1 NM15:1 M95:1 ENDF:4 MK:16 NC8:8 DUMPI:8 DUMPL:8".split():
+    PART[_n.split(":")[0]] = _at
+    _at += int(_n.split(":")[1])
+SCRATCH["CF"] = ("sbuf", [128, _at], "float32")
+SEMAPHORES = ["sv", "ss", "sp", "sg", "ls", "za1", "za2", "zr"] + ["d%d" % i for i in range(14)]
+TWO = ("bfloat16", "float16", "uint16")
+COSTS = [dict(cy=1.0, pe=0.5, ga=1.5, sc=3.0, wake=60.0, same=40.0, dma=2000.0, bw=200.0, rem=2500.0),
+         dict(cy=0.9, pe=0.5, ga=1.15, sc=2.0, wake=110.0, same=60.0, dma=2000.0, bw=250.0, rem=3500.0),
+         dict(cy=1.15, pe=0.6, ga=1.95, sc=5.0, wake=60.0, same=40.0, dma=2200.0, bw=150.0, rem=2000.0)]
+TRIALS = 5000
+GW, GO, YW = "SWWS", (1, 0, 2, 3), "SVVV"
+ORDER = {}
+
+
+def R(buf, c0, c1, step=1, p0=0, p1=128):
+    if buf in PART:
+        return ("CF", PART[buf] + c0, PART[buf] + c1, step, p0, p1)
+    return (buf, c0, c1, step, p0, p1)
+
+
+def ind(win, off): return ("ind", win, off)
+def wid(r): return 16 * (r[2][2] - r[2][1]) if len(r) == 3 else (r[2] - r[1] + r[3] - 1) // r[3]
+def kind(r): return SCRATCH[(r[1] if len(r) == 3 else r)[0]][2]
+
+
+def schedule(ops):
+    n = len(ops)
+    rnd = [12345]
+
+    def rand():
+        rnd[0] = (rnd[0] * 1103515245 + 12345) & 0x7fffffff
+        return (rnd[0] >> 8) / 0x7fffff
+
+    que = [o["q"] for o in ops]
+    succ = [[] for _ in range(n)]
+    pred = [list(o["pre"].items()) for o in ops]
+    for i in range(n):
+        for j, w in pred[i]: succ[j].append((i, w))
+    cost, lat, hop = [], [], []
+    for C in COSTS:
+        cost.append([o["f"][0] + C["cy"] * (o["f"][1] + C["ga"] * o["f"][2] + C["sc"] * o["f"][3]) + C["pe"] * o["f"][4] for o in ops])
+        lat.append([o["lat"][0] * C["dma"] + o["lat"][1] / C["bw"] + o["lat"][2] * C["rem"] for o in ops])
+        hop.append((C["wake"], C["same"]))
+
+    def length(order, s):
+        c, la, (wk, sm) = cost[s], lat[s], hop[s]
+        fin, sta, free, end = [0.0] * n, [0.0] * n, {}, 0.0
+        for i in order:
+            q = que[i]
+            t = free.get(q, 0.0)
+            for j, w in pred[i]:
+                a = (fin[j] + (sm if que[j] == q else wk)) if w else sta[j]
+                if a > t: t = a
+            sta[i] = t
+            free[q] = t + c[i]
+            fin[i] = t + c[i] + la[i]
+            if fin[i] > end: end = fin[i]
+        return end
+
+    pri = [0.0] * n
+    for i in range(n - 1, -1, -1):
+        pri[i] = cost[0][i] + lat[0][i]
+        for k, w in succ[i]:
+            d = cost[0][i] + (lat[0][i] + hop[0][que[k] == que[i]] if w else 0)
+            if d + pri[k] > pri[i]: pri[i] = d + pri[k]
+
+    def greedy(key, look):
+        c, la, (wk, sm) = cost[0], lat[0], hop[0]
+        left = [len(p) for p in pred]
+        ready, rt, free, order = {}, [0.0] * n, {}, []
+        for i in range(n):
+            if not left[i]: ready.setdefault(que[i], []).append(i)
+        while len(order) < n:
+            bq, bt = None, 1e18
+            for q, L in ready.items():
+                if L:
+                    t = max(free.get(q, 0.0), min([rt[i] for i in L]))
+                    if t < bt: bq, bt = q, t
+            L = ready[bq]
+            best = max([i for i in L if rt[i] <= bt + look], key=lambda i: key[i])
+            L.remove(best)
+            s = max(bt, rt[best])
+            e = s + c[best]
+            free[bq] = e
+            order.append(best)
+            e += la[best]
+            for k, w in succ[best]:
+                a = (e + (sm if que[k] == bq else wk)) if w else s
+                if a > rt[k]: rt[k] = a
+                left[k] -= 1
+                if not left[k]: ready.setdefault(que[k], []).append(k)
+        return order
+
+    best = (1e18, None, None, 0.0)
+    for it in range(TRIALS):
+        if it <= TRIALS // 5:
+            amp = 0.0 if it == 0 else 2000.0 * rand()
+            key = [p + amp * (rand() - 0.5) for p in pri]
+            look = 0.0 if it == 0 else 400.0 * rand()
+        else:
+            key, look = list(best[2]), best[3]
+            share = 0.01 if rand() < 0.5 else 0.06
+            for i in range(n):
+                if rand() < share: key[i] += 4000.0 * (rand() - 0.5)
+            if rand() < 0.2: look = 400.0 * rand()
+        order = greedy(key, look)
+        if it == 0: base = [length(order, s) for s in range(len(COSTS))]
+        e = sum([length(order, s) / base[s] for s in range(len(COSTS))])
+        if e < best[0]: best = (e, order, key, look)
+    return length(best[1], 0), best[1]
+
+
+def make(g, T):
+    eng = {"V": g.vector, "S": g.scalar, "P": g.tensor, "G": g, "Y": g.sync}
+    own = {"V": "sv", "S": "ss", "P": "sp", "G": "sg"}
+    ops, hist = [], {}
+
+    def ap(r):
+        if len(r) == 3:
+            return ap(r[1]).indirect(ap(r[2]))
+        b, c0, c1, s, p0, p1 = r
+        return T[b][p0:p1, c0:c1] if s == 1 else T[b][p0:p1, c0:c1:s]
+
+    def add(q, outs, ins, call, f, lat=(0, 0, 0), sem=None, inc=1, extra=()):
+        i = len(ops)
+        acc = []
+        for r in ins:
+            if isinstance(r, tuple):
+                acc += [(r[1], False), (r[2], False)] if len(r) == 3 else [(r, False)]
+        for r in outs:
+            acc += [(r[1], True), (r[2], False)] if len(r) == 3 else [(r, True)]
+        pre = {j: True for j in extra}
+        for r, w in acc:
+            ps = r[0] in PSUM
+            h = hist.setdefault(r[0], [])
+            for (j, r2, w2) in h:
+                if j == i: continue
+                q2 = ops[j]["q"]
+                if ps:
+                    if q == q2 == "P": wait = False
+                    elif q == q2 and not (w or w2): continue
+                    else: wait = not (q == q2 and not w2)
+                else:
+                    if not (w or w2) or r[1] >= r2[2] or r2[1] >= r[2] or r[4] >= r2[5] or r2[4] >= r[5]: continue
+                    if r[3] == r2[3] and r[3] > 1 and (r[1] - r2[1]) % r[3]: continue
+                    wait = not (q == q2 and not w2)
+                pre[j] = pre.get(j, False) or wait
+            if ps and q == "P": h[:] = []
+            elif w and not ps and r[3] == 1:
+                h[:] = [a for a in h if a[0] == i or not (a[1][1] >= r[1] and a[1][2] <= r[2] and a[1][4] >= r[4] and a[1][5] <= r[5])]
+            h.append((i, r, w))
+        ops.append(dict(q=q, call=call, f=tuple(f) + (0,) * (5 - len(f)), lat=lat, pre=pre, sem=sem or own.get(q), inc=inc))
+        return i
+
+    def sc(x): return ap(x) if isinstance(x, tuple) else x
+
+    def vcost(out, in_, f):
+        n = wid(out)
+        if len(out) == 3: return (50, 0, 0, n)
+        if len(in_) == 3: return (50, 0, n)
+        return (0, max(64, n * f))
+
+    def half(*rs): return 0.5 if all(kind(r) in TWO for r in rs) else 1.0
+
+    def cp(out, in_): add("V", [out], [in_], lambda n: n.tensor_copy(ap(out), ap(in_)), vcost(out, in_, half(out, in_)))
+
+    def tt(out, a, b, o):
+        add("V", [out], [a, b], lambda n: n.tensor_tensor(ap(out), ap(a), ap(b), o), vcost(out, a, 1.0 if a[0] in PSUM or b[0] in PSUM else 2.0))
+
+    def ts(out, a, s1, o1, s2=None, o2=None):
+        c = vcost(out, a, half(out, a))
+        if o2 is None: add("V", [out], [a, s1], lambda n: n.tensor_scalar(ap(out), ap(a), sc(s1), None, o1), c)
+        else: add("V", [out], [a, s1, s2], lambda n: n.tensor_scalar(ap(out), ap(a), sc(s1), sc(s2), o1, o2), c)
+
+    def scan(out, a, b, o1, o2):
+        add("V", [out], [a, b], lambda n: n.tensor_tensor_scan(ap(out), ap(a), ap(b), 0.0, o1, o2), vcost(out, a, half(out, a, b)))
+
+    def fill(out, v): add("V", [out], [], lambda n: n.memset(ap(out), v), vcost(out, out, half(out)))
+
+    def act(out, in_, f, bias=0.0, scale=1.0, acc=None):
+        c = (65, 0, wid(out)) if len(in_) == 3 else (0 if acc is None else 20, max(64, wid(out)))
+        if acc is None: add("S", [out], [in_, bias, scale], lambda n: n.activation(ap(out), ap(in_), f, bias=sc(bias), scale=sc(scale)), c)
+        else: add("S", [out, acc], [in_, bias, scale], lambda n: n.activation(ap(out), ap(in_), f, bias=sc(bias), scale=sc(scale), accum_out=ap(acc)), c)
+
+    def mm(*group):
+        def call(n):
+            for (o, l, r, a, b) in group:
+                x = n.matmul(ap(o), ap(l), ap(r), a, b)
+            return x
+        c = sum(max(min(64, wid(l)), wid(r)) * (4 if kind(l) == "float32" else 1) for (o, l, r, a, b) in group)
+        add("P", [x[0] for x in group], [x[1] for x in group] + [x[2] for x in group], call, (0, 0, 0, 0, c))
+
+    def iota(out, pat, base, cm): add("G", [out], [], lambda n: n.iota(ap(out), pat, base, cm, allow_small_or_imprecise_dtypes=True), (130, 2 * wid(out)))
+    def asel(out, in_, pat, o, fillv, base, cm): add("G", [out], [in_], lambda n: n.affine_select(ap(out), ap(in_), pat, o, fillv, base, cm), (170, 2 * wid(out)))
+
+    def cast(out, in_): asel(out, in_, [[0, wid(out)]], ALU.is_gt, 0.0, 1, 0)
+
+    nd = [0]
+
+    def dma(q, out, in_):
+        sem = "d%d" % nd[0]
+        nd[0] += 1
+        o = T[out][:] if isinstance(out, str) else ap(out)
+        i = T[in_][:] if isinstance(in_, str) else ap(in_)
+        s = in_ if isinstance(out, str) else out
+        by = wid(s) * 128 * (2 if kind(s) in TWO else 4)
+        add(q, [] if isinstance(out, str) else [out], [] if isinstance(in_, str) else [in_], lambda n: n.dma_start(o, i), (60,), (1, by, 0), sem, 16)
+
+    def send(out, in_, rsem, dst, src, topo):
+        rid, pid, _ = topo.addr(dst)
+        en = topo.engines(src, dst)[:8]
+        i = add("G", [], [in_], lambda n: n.remote_dma(ap(out), ap(in_), T.sem[rsem], T.sem["ls"], pid, rid, sum(1 << x for x in en)), (1000,), (0, 0, 1), "ls", len(en))
+        add("net", [out], [], None, (0,), (0, 0, 0), rsem, len(en), (i,))
+
+    def run():
+        if not ORDER:
+            ORDER["best"] = schedule(ops)
+        cnt, known, tok = {}, {q: {} for q in eng}, {}
+        for i in ORDER["best"][1]:
+            o = ops[i]
+            q = o["q"]
+            cnt[o["sem"]] = cnt.get(o["sem"], 0) + o["inc"]
+            if q == "net":
+                tok[i] = (o["sem"], cnt[o["sem"]], {})
+                continue
+            k = known[q]
+            waits = sorted((tok[j] for j, w in o["pre"].items() if w), key=lambda t: (t[0], -t[1]))
+            waits.sort(key=lambda t: t[0] == o["sem"])
+            for (s, v, snap) in waits:
+                if k.get(s, 0) < v:
+                    eng[q].wait_ge(T.sem[s], v)
+                    k[s] = v
+                    for a, b in snap.items():
+                        if k.get(a, 0) < b: k[a] = b
+            c = o["call"](eng[q])
+            if o["sem"] != "ls": c.then_inc(T.sem[o["sem"]], o["inc"])
+            tok[i] = (o["sem"], cnt[o["sem"]], dict(k))
+        for s in sorted(cnt):
+            if known["G"].get(s, 0) < cnt[s]: g.wait_ge(T.sem[s], cnt[s])
+
+    return dict(cp=cp, tt=tt, ts=ts, scan=scan, fill=fill, act=act, mm=mm, iota=iota, asel=asel, cast=cast, dma=dma, send=send, run=run)
+
+
+def rank_program(g, core, T, topo):
+    rank = T.rank_of(core)
+    if rank is None:
+        return
+    n = len(T.cores)
+    m = make(g, T)
+    cp, tt, ts, scan, fill, act, mm, iota, asel, cast, dma = (m[k] for k in ("cp", "tt", "ts", "scan", "fill", "act", "mm", "iota", "asel", "cast", "dma"))
+    F = lambda b: R(b, 0, SCRATCH[b][1][1])
+    C = lambda b, i=0: R(b, i, i + 1)
+    S8 = lambda i: R("WLF", 8 * i, 8 * i + 8)
+    K8 = lambda i: R("KJ", 8 * i, 8 * i + 8)
+    D8 = lambda b: R(b, 0, 8)
+    G8 = lambda i: R("G8", 8 * i, 8 * i + 8)
+    C8 = G8(2)
+    PU, PP, PQ, PZ = R("p0", 0, 128), R("p0", 128, 256), R("p0", 256, 384), R("p0", 384, 512)
+    KEY, E8, REC8, AA = R("p1", 0, 128), R("p1", 128, 136), R("p1", 136, 144), R("p1", 144, 145)
+    CNT, CNB, JJB = R("p3", 128, 256), R("p3", 256, 384), R("p3", 384, 512)
+    ST, FT = R("p4", 128, 256), R("p4", 256, 384)
+    J8, CN8 = R("p7", 96, 104), R("p7", 104, 112)
+    HP, DP, JNP = R("p7", 128, 256), R("p7", 256, 384), R("p7", 384, 512)
+    WI, WL, WX, WG = F("IX"), F("LK"), F("XC"), F("GI")
+
+    dma("Y", F("Z0"), "zc"); dma("Y", F("WTI"), "wt"); dma("Y", F("HKI"), "hk")
+    dma("S", R("GI", 0, 1024), "gi"); dma("Y", F("IXI"), "ix"); dma("Y", F("THI"), "th"); dma("S", F("XC"), "xc"); dma("Y", F("LKI"), "lk")
+
+    fill(F("ONES"), 1.0)
+    iota(F("PIO"), [[0, 16]], 0, 1)
+    asel(F("IDF"), F("ONES"), [[-1, 128]], ALU.is_equal, 0.0, 0, 1)
+    asel(F("BOF"), F("ONES"), [[-16, 8], [0, 16]], ALU.is_ge, 0.0, 0, 1)
+    asel(F("BOF"), F("BOF"), [[16, 8], [0, 16]], ALU.is_ge, 0.0, 15, -1)
+    iota(F("RQ"), [[0, 8], [1, 16]], 0, 0)
+    iota(F("CIO"), [[1, 8]], 0, 0)
+    asel(F("SHF"), F("ONES"), [[-1, 128]], ALU.is_equal, 0.0, -1, 1)
+    asel(F("UT"), F("BOF"), [[1, 128]], ALU.is_ge, 0.0, 0, -1)
+    fill(R("ZS", 512, 1536), 0.0)
+    for h in (0, 1):
+        fill(R("RX", 1024 * h, 1024 * h + 1024), 1.0)
+    fill(R("RX", 0, 2048, 16), 0.0)
+    fill(F("ONESB"), 1.0)
+    fill(F("EB"), 0.0)
+    for q in (0, 3, 1, 2):
+        asel(R("RM", 512 * q, 512 * q + 512), F("ONESB"), [[-1, 32], [0, 16]], ALU.is_equal, 0.0, -32 * q, 1)
+    for c in range(8):
+        act(R("R1", SEG[c], SEG[c + 1]), R("IDF", 0, 16 * c + 16), ACT.Copy)
+    ts(F("PR"), F("PIO"), 15, ALU.bitwise_and)
+    act(F("BOB"), F("BOF"), ACT.Copy)
+    cp(C("RF"), C("PR"))
+    act(F("IDB"), F("IDF"), ACT.Copy)
+    act(F("NIDB"), F("IDF"), ACT.Copy, scale=-1.0)
+    cp(C("WC"), C("WTI"))
+    ts(F("WB"), F("BOF"), C("WC"), ALU.mult)
+    cp(R("HKF", 0, 2), F("HKI"))
+    ts(F("PD"), F("IDF"), C("HKF", 0), ALU.mult)
+    ts(F("QD"), F("IDF"), C("HKF", 1), ALU.mult)
+    PA, PB = R("p1", 128, 256), R("p1", 256, 384)
+    mm((PA, F("BOB"), F("PD"), True, True), (PB, F("BOB"), F("QD"), True, True))
+    ts(F("PWI"), PA, C("WC"), ALU.mult)
+    ts(F("QWI"), PB, C("WC"), ALU.mult)
+    ts(F("PWI"), F("PWI"), 1023, ALU.bitwise_and)
+    ts(F("QWI"), F("QWI"), 2047, ALU.bitwise_and)
+    cp(F("PW"), F("PWI"))
+    cp(F("QW"), F("QWI"))
+    ts(F("M16"), F("RQ"), C("RF"), ALU.is_equal)
+    ts(F("RMIN"), F("RQ"), 0.0, ALU.is_equal, 3.0e7, ALU.mult)
+    ts(F("RMAX"), F("RMIN"), -2.0, ALU.mult, 3.0e7, ALU.add)
+    for i, v in enumerate((16384.0, 32768.0, 1.0, -0.5, None, -16384.0, 65536.0, -32768.0)):
+        if v is not None: act(G8(i), R("BOF", 0, 128, 16), ACT.Copy, scale=v)
+    cp(F("OFFG"), F("CIO"))
+    act(F("MROW"), F("RQ"), ACT.Copy, scale=1024.0)
+    ts(C("JJC"), C("RF"), -2048.0, ALU.mult, 30720.0, ALU.add)
+    fill(R("IX", 1024, 1152), 0.0)
+    fill(R("LK", 2048, 2192), 0.0)
+    fill(R("GI", 1024, 1152), 0.0)
+    fill(R("XG", 2048, 2064), 0.0)
+    act(F("M16B"), F("M16"), ACT.Copy)
+    for k in range(0, 16, 4):
+        asel(R("SEL", 128 * k, 128 * k + 512), F("ONESB"), [[-1, 4], [-1024, 8], [-63, 16]], ALU.is_equal, 0.0, -k, 64)
+    for at, v in ((0, 1.0), (144, 2.0), (288, -1.0)):
+        act(R("EB", at + 15, at + 143, 16), R("BOF", 0, 128, 16), ACT.Copy, scale=v)
+    ts(D8("NC8"), R("BOF", 0, 128, 16), -1.0, ALU.mult)
+    for c in range(8):
+        act(R("R2", SEG[c], SEG[c + 1]), R("ONESB", 0, 16 * c + 16), ACT.Copy, scale=C("NC8", c))
+    fill(F("R3"), 0.0)
+    for c in range(8):
+        act(R("R3", SEG[c + 1] - 16, SEG[c + 1]), R("UT", 16 * c, 16 * c + 16), ACT.Copy, scale=4096.0)
+    fill(F("RD"), 0.0)
+    for c in range(8):
+        fill(C("RD", SEG[c]), 1.0e6)
+    ts(C("ENDF", 0), C("RF"), 7.0, ALU.min)
+    ts(C("ENDF", 1), C("ENDF", 0), 8.0, ALU.mult, 24.0, ALU.add)
+    tt(C("ENDF", 2), C("ENDF", 0), C("ENDF", 1), ALU.mult)
+    ts(C("ENDS"), C("ENDF", 2), 15.0, ALU.add)
+    ts(D8("DUMPI"), F("CIO"), 16.0, ALU.mult, C("RF"), ALU.add)
+    ts(D8("DUMPL"), D8("DUMPI"), 2049.0, ALU.add)
+    ts(D8("DUMPI"), D8("DUMPI"), 1024.0, ALU.add)
+    ts(F("MNEG"), F("M16"), 128.0, ALU.mult, -128.0, ALU.add)
+    cp(R("THF", 0, 2), F("THI"))
+    ts(C("NM15"), C("RF"), 15.0, ALU.is_equal, 2000.0, ALU.mult)
+    tt(C("ACOL"), C("THF", 0), C("NM15"), ALU.subtract)
+    ts(C("BCOL"), C("THF", 1), -1.0, ALU.mult, 1023.5, ALU.add)
+    act(F("HID"), F("IDF"), ACT.Copy, scale=0.5)
+    act(F("NHID"), F("IDF"), ACT.Copy, scale=-0.5)
+    act(F("IDK"), F("IDF"), ACT.Copy, scale=512.0)
+    act(F("NID4K"), F("IDF"), ACT.Copy, scale=-4096.0)
+    act(F("SHB"), F("SHF"), ACT.Copy)
+    fill(G8(4), -7.0)
+    fill(F("M24"), -16777216.0)
+    fill(F("HALF"), 0.5)
+    fill(C("M95"), -9.5)
+    for h in (0, 512):
+        cast(R("IX", h, h + 512), R("IXI", h, h + 512))
+
+    def ustage(t):
+        z = F("Z%d" % t)
+        if t: mm((PU, F("WB"), z, True, True), (PP, F("PW"), z, True, True), (PQ, F("QW"), z, True, True))
+        else: mm((PU, F("WB"), z, True, True))
+        cp(F("UI"), PU)
+        if not t: mm((PP, F("PW"), z, True, True))
+        if not t: mm((PQ, F("QW"), z, True, True))
+        ts(F("UI"), F("UI"), 4095, ALU.bitwise_and)
+        tt(F("UU"), F("UI"), F("UI"), ALU.mult)
+        ts(F("S5"), F("UU"), 5, ALU.arith_shift_right, 1023, ALU.bitwise_and)
+        tt(F("BS"), PP, F("S5"), ALU.add)
+        ts(F("VQ"), F("UU"), 4, ALU.arith_shift_right, 2047, ALU.bitwise_and)
+        tt(F("VQ"), PQ, F("VQ"), ALU.add)
+        ts(F("VQ"), F("VQ"), 2047, ALU.bitwise_and)
+        cp(F("VH"), F("VQ"))
+        cp(R("ZS", 512, 1536, 16), R("Z%d" % t, 32, 96))
+        scan(R("ZREP", 512, 1536), R("RX", 512, 1536), R("ZS", 512, 1536), ALU.mult, ALU.add)
+        mm((R("p0", 384, 512), z, F("NIDB"), True, True))
+        act(F("ZT%d" % (t & 1)), R("p0", 384, 512), ACT.Copy)
+
+    def estage(t):
+        b = F("BS")
+        if t:
+            ts(F("EI"), b, AA, ALU.add, 8192.0, ALU.add)
+            b = F("EI")
+        ts(F("EM"), b, 1023, ALU.bitwise_and)
+        cp(F("EU"), F("EM"))
+        cast(F("MKEY"), F("EM"))
+        mm((KEY, F("MKEY"), F("IDF"), True, False))
+
+    def zsub(p, t, a, b): return (p, F("ZT%d" % (t & 1)), R("RM", a, b), True, False)
+
+    def dist(win, off, sub, sh, who, t=None):
+        bank = ["p2", "p5" if sub == "ZREP" else "p6"]
+        DG, AG = ("DG", "AG") if sub == "ZREP" else ("DY", "AY")
+        for q in range(4):
+            a, b = 512 * q, 512 * q + 512
+            if who[q] == "S":
+                p = bank.pop(0)
+                x = 512 * (p != "p2")
+                act(R("GR", x, x + 512), ind(win, R(off, 32 * q, 32 * q + 32)), ACT.Copy)
+                P = R(p, 0, 512)
+                if sub == "ZREP": mm(zsub(P, t, a, b))
+                else: mm((P, F("NIDB"), R(sub, a + sh, b + sh), True, False))
+                mm((P, F("IDB"), R("GR", x, x + 512), False, True))
+                act(R(AG, a, b), R(p, 0, 512), ACT.Abs)
+            else:
+                tt(R(DG, a, b), ind(win, R(off, 32 * q, 32 * q + 32)), R(sub, a + sh, b + sh), ALU.subtract)
+                if who[q] == "V": act(R(AG, a, b), R(DG, a, b), ACT.Abs)
+                else: ts(R(AG, a, b), R(DG, a, b), 0.0, ALU.max)
+
+    def runs(who):
+        out = []
+        for q in range(4):
+            w = who[q] == "W"
+            if q % 2 and out[-1][2] == w: out[-1] = (out[-1][0], q + 1, w)
+            else: out.append((q, q + 1, w))
+        return out
+
+    def lanesum(out, who, pieces, ks, one, two, neg):
+        for (a, b, w) in pieces:
+            x = "G" if out[0] == "p1" else "Y"
+            for (buf, wt) in ((("D" + x, neg), ("A" + x, two)) if w else (("A" + x, one),)):
+                mm(*[(R(out[0], out[1] + k, out[1] + 128, 16, 32 * a, 32 * b), R(buf, 512 * a + k, 512 * b, 16), wt, False, False) for k in ks])
+
+    def gstage(t):
+        dist(WG, "EU", "ZREP", 0, GW, t)
+        for q in GO:
+            lanesum(("p1", 0), GW, [(q, q + 1, GW[q] == "W")], range(16), G8(0), G8(1), G8(5))
+        mm((KEY, F("IDB"), F("MROW"), False, True))
+
+    def argstage(t):
+        scan(F("KMIN"), F("RMIN"), KEY, ALU.max, ALU.min)
+        ts(F("KA"), R("KMIN", 15, 128, 16), 1023, ALU.bitwise_and)
+        tt(F("ERM"), ind(F("KA"), F("OFFG")), F("M16"), ALU.mult)
+        mm((E8, F("ERM"), C8, True, True))
+        cp(F("E8U"), E8)
+        cp(F("JU"), ind(F("IXI") if t == 0 else WI, F("E8U")))
+        act(F("JJ%d" % (t & 1)), ind(WI, F("E8U")), ACT.Identity, bias=C("JJC"))
+        cp(F("JH"), F("JU"))
+
+    def lkx(t):
+        lk = F("LKI") if t == 0 else WL
+        for h in (0, 1):
+            L = 1024 * h
+            cp(R("LG", L, L + 1024), ind(lk, R("JU", 64 * h, 64 * h + 64)))
+            p = R(("p3", "p4")[h], 0, 64)
+            mm(*[(p, R("SEL", 128 * k, 128 * k + 128), R("LG", L + k, L + 1024, 16), k == 0, k == 15) for k in range(16)])
+            cp(R("NU", 64 * h, 64 * h + 64), p)
+        for q in range(4):
+            act(R("XG", 512 * q, 512 * q + 512), ind(WX, R("JU", 32 * q, 32 * q + 32)), ACT.Copy)
+
+    def pairs(masked, plain):
+        for (a, b, P) in ((0, 512, R("p6", 0, 512)), (512, 576, R("p7", 0, 64))):
+            mm((P, F("M16B"), R("R3", a, b), True, False), (P, F(plain), R("R1", a, b), False, False), (P, F(masked), R("R2", a, b), False, True))
+            act(R("XA", a, b), P, ACT.Abs)
+
+    def lost(out16):
+        scan(F("XS"), F("RD"), F("XA"), ALU.max, ALU.min)
+        ts(out16, ind(F("XS"), C("ENDS")), 0.0, ALU.is_le)
+
+    def idx(t):
+        cp(F("ERU"), ind(F("KA"), F("OFFG")))
+        pairs("ERM", "ERU")
+        lost(R("WLF", 16, 32))
+        tt(S8(0), S8(2), D8("DUMPI"), ALU.mult)
+        tt(S8(0), E8, S8(0), ALU.max)
+        cp(F("NOFF"), S8(0))
+
+    def znext(t):
+        for h in (0, 1024):
+            scan(R("XM", h, h + 1024), R("RX", h, h + 1024), R("XG", h, h + 1024), ALU.mult, ALU.max)
+        mm((PZ, F("IDB"), F("Z%d" % t), True, False), (PZ, F("IDB"), R("XM", 15, 2048, 16), False, True))
+        act(F("ZH"), PZ, ACT.Copy, bias=129.75, scale=0.5)
+        act(F("ZN%d" % t), F("ZH"), ACT.Copy, bias=-130.0)
+        if t < RO - 1:
+            m["send"](F("Z%d" % (t + 1)), F("ZN%d" % t), "za%d" % (t + 1), T.cores[(rank + 1) % n], core, topo)
+        else:
+            m["send"](F("ZR"), F("ZN%d" % t), "zr", T.cores[(rank - t) % n], core, topo)
+
+    def far(t):
+        P = R("p5", 0, 512)
+        for q in range(4):
+            a, b = 512 * q, 512 * q + 512
+            mm(zsub(P, t, a, b), (P, F("IDB"), R("XG", a, b), False, True))
+            act(R("AF", a, b), P, ACT.Abs)
+
+    def ystage(t):
+        dist(WX, "NU", "XG", 1, YW)
+        for (a, b, w) in runs(YW):
+            o = R("p4", 128 + 32 * a, 128 + 32 * b)
+            src = (("DY", 288), ("AY", 144)) if w else (("AY", 0),)
+            for i, (buf, at) in enumerate(src):
+                mm(*[(o, R("EB", at + 15 - k, at + 143 - k), R(buf, 512 * a + k, 512 * b, 16), i == 0 and k == 0, i == len(src) - 1 and k == 14) for k in range(15)])
+
+    def rec(t):
+        ts(F("CMP"), ST, C("ACOL"), ALU.is_le)
+        if t < RO - 1:
+            mm((CNT, F("IDB"), F("MNEG"), True, False), (CNT, F("CMP"), F("BOB"), False, True))
+            act(F("RECS"), CNT, ACT.Sign, bias=C("M95"), acc=F("ACC"))
+            mm((REC8, F("IDB"), G8(4), True, False), (REC8, F("RECS"), G8(3), False, True), (AA, F("HALF"), F("ACC"), True, True))
+        mm((CN8, F("CMP"), C8, True, True))
+        mm((CNB, F("BOB"), F("CMP"), True, True))
+
+    def gists(t):
+        tt(S8(4), REC8, D8("DUMPI"), ALU.mult)
+        tt(F("GOFF"), S8(4), S8(0), ALU.max)
+        cp(ind(WG, F("GOFF")), F("Z%d" % t))
+
+    def names(t):
+        mm((HP, F("HID"), F("VH"), True, False), (HP, F("HID"), F("JH"), False, True), (DP, F("HID"), F("VH"), True, False), (DP, F("NHID"), F("JH"), False, True))
+        act(F("HV"), HP, ACT.Copy)
+        act(F("RBS"), CNB, ACT.Sign, bias=C("M95"))
+        mm((FT, F("IDK"), F("RBS"), True, False))
+        for h in (0, 1):
+            mm(*[(R("p4", 256 + 64 * h, 320 + 64 * h), R("EB", 15 - k, 143 - k), R("AF", 1024 * h + k, 1024 * h + 1024, 16), False, False) for k in range(16)])
+        mm((FT, F("IDK"), F("RBS"), False, True))
+        act(F("SG"), FT, ACT.Sign, bias=C("BCOL"))
+        tt(F("NT"), DP, F("SG"), ALU.mult)
+        tt(ind(WI, F("NOFF")), F("HV"), F("NT"), ALU.add)
+
+    def links(t):
+        JJ = F("JJ%d" % (t & 1))
+        mm((PZ, F("IDB"), F("M24"), True, False))
+        lanesum(("p0", 384), YW, runs(YW), range(15), G8(1), G8(6), G8(7))
+        mm((PZ, JJ, F("IDF"), False, True))
+        scan(F("KMX"), F("RMAX"), PZ, ALU.min, ALU.max)
+        ts(K8(0), R("KMX", 15, 128, 16), 32767, ALU.bitwise_and)
+        ts(K8(1), R("KMX", 15, 128, 16), 2047, ALU.bitwise_and)
+        ts(S8(5), CN8, 10.0, ALU.is_ge, 2048.0, ALU.mult)
+        tt(K8(2), K8(1), S8(5), ALU.max)
+        cast(S8(7), K8(0))
+        act(F("REP2"), ind(S8(7), F("OFFG")), ACT.Copy)
+        mm((JJB, F("REP2"), F("IDF"), True, True))
+        tt(F("ERM2"), ind(K8(2), F("OFFG")), F("M16"), ALU.mult)
+        mm((J8, F("ERM2"), C8, True, True))
+        cp(F("ERU2"), ind(K8(2), F("OFFG")))
+        pairs("ERM2", "ERU2")
+        tt(F("NOH"), JJB, JJ, ALU.not_equal)
+        act(F("NOHB"), F("NOH"), ACT.Copy)
+        mm((JNP, F("SHB"), F("JH"), True, False), (JNP, F("NID4K"), F("NOHB"), False, True))
+        act(F("JN"), JNP, ACT.Copy)
+        cp(F("JX8"), J8)
+        tt(F("TOLD"), ind(WL, F("JX8")), F("NOH"), ALU.mult)
+        lost(R("WLF", 16, 32))
+        tt(S8(6), S8(2), D8("DUMPL"), ALU.mult)
+        tt(F("LOFF"), J8, S8(6), ALU.max)
+        tt(ind(WL, F("LOFF")), F("TOLD"), F("JN"), ALU.max)
+
+    ustage(0)
+    estage(0)
+    for t in range(RO):
+        gstage(t)
+        argstage(t)
+        lkx(t)
+        if t == 0:
+            for h in range(0, 2048, 512):
+                cast(R("LK", h, h + 512), R("LKI", h, h + 512))
+        idx(t)
+        znext(t)
+        ystage(t)
+        rec(t)
+        if t < RO - 1: gists(t)
+        far(t)
+        names(t)
+        links(t)
+        if t < RO - 1:
+            ustage(t + 1)
+            estage(t + 1)
+    dma("S", "yi", R("IX", 0, 1024))
+    dma("Y", "yl", R("LK", 0, 2048))
+    dma("Y", "yz", F("ZR"))
+    m["run"]()

@@ -1,4 +1,4 @@
-from concourse.mybir import AluOpType, ActivationFunctionType
+from concourse.mybir import AluOpType, ActivationFunctionType, AxisListType
 
 ALU = AluOpType
 ACT = ActivationFunctionType
@@ -7,30 +7,30 @@ SEG = [8 * c * (c + 1) for c in range(9)]
 PSUM = ("p0", "p1", "p2", "p3", "p4", "p5", "p6", "p7")
 SCRATCH = {b: ("psum", [128, 512], "float32") for b in PSUM}
 for _t, _names in {
-    "float32": "IX:1152 LK:2192 ONES:128 IDF:128 BOF:128 SHF:128 HALF:128 RQ:128 M16:128 RMIN:128 RMAX:128 UT:128 MKEY:128 JJ0:128 JJ1:128 ACC:1 WLF:64 SG:128 HV:128 "
-               "NT:128 REP2:128 NOH:128 JN:128 TOLD:128",
-    "bfloat16": "XC:2048 GI:1152 Z0:128 Z1:128 Z2:128 ZR:128 ZN0:128 ZN1:128 ZN2:128 ZH:128 ZS:2048 ZREP:2048 ZT0:128 ZT1:128 RM:2048 ONESB:512 IDB:128 NIDB:128 HID:128 NHID:128 IDK:128 "
-                "NID4K:128 BOB:128 SHB:128 EB:432 G8:64 MROW:128 M24:128 M16B:128 MNEG:128 SEL:2048 RX:2048 RD:576 R1:576 R2:576 R3:576 WB:128 "
-                "DG:2048 AG:2048 DY:2048 AY:2048 GR:1024 XG:2064 XM:2048 CMP:128 RECS:128 RBS:128 XA:576 XS:576 AF:2048 NOHB:128",
-    "float16": "PD:128 QD:128 PW:128 QW:128 VH:128 ERM:128 ERU:128 ERM2:128 ERU2:128 JH:128 LG:2048",
-    "int32": "IXI:1024 LKI:2048 WTI:1 HKI:2 THI:2 PIO:16 PR:16 CIO:8 PWI:128 QWI:128 UI:128 UU:128 S5:128 BS:128 VQ:128 EI:128 EM:128 KMIN:128 KA:8 KMX:128 KJ:24",
-    "uint16": "OFFG:8 ENDS:2 EU:128 E8U:8 JU:128 NU:128 GOFF:8 NOFF:8 LOFF:8 JX8:8",
+    "float32": "IX:1152 LK:2176 IDF:128 W16:128 UU:128 THR:128 ACC:1 WLF:64 KE:8 DUMP:16 TW:32 ERF:128 ERF2:128 NA:256 LA:256 TOLD:128",
+    "bfloat16": "XC:2048 GI:1152 Z0:128 Z1:128 Z2:128 ZR:128 ZN0:128 ZN1:128 ZN2:128 ZH:128 ZS:2048 ZREP:2048 ZT0:128 ZT1:128 RM:512 MK:1024 RX:1024 RD:576 XA:576 XS:576 J32:512 "
+                "ONESB:128 DIF:144 RQ:128 HQ:128 IDB:144 NIDB:128 P4K:128 N4K:128 HID:128 BOB:128 M16:128 TH16:128 RS:128 RC:128 CRI:128 CRL:128 UT:128 "
+                "G8:64 R1:576 R2:576 WB:128 QB:128 DG:2048 AG:2048 DY:2048 AY:2048 GR:1024 XG:2064 XM:2048 AF:2048 CMP:128 CNS:128 RS8:8 NRM:128 SG:128 STEP:144",
+    "float16": "PD:128 QD:128 TD:128 TB:128 DL:8 PW:128 QW:128 VH0:128 VH1:128 EH:128 ERM:128 ERU:128 ERM2:128 ERU2:128 JH0:128 JH1:128 LG:2048",
+    "int32": "IXI:1024 LKI:2048 WTI:1 HKI:2 THI:2 PIO:1 PR:3 CIO:32 PWI:128 QWI:128 VI:128 EI:128 KMIN:128 KA:8 KMX:128 KJ:8",
+    "uint16": "OFFG:16 ENDS:2 EU:128 E8U:8 JU:128 NU:128 GOFF:8 NOFF:8 LOFF:8 JX8:8",
 }.items():
     for _n in _names.split():
         SCRATCH[_n.split(":")[0]] = ("sbuf", [128, int(_n.split(":")[1])], _t)
 PART = {}
 _at = 0
-for _n in "RF:1 WC:1 HKF:2 ACOL:1 BCOL:1 THF:2 JJC:1 NM15:1 M95:1 ENDF:4 MK:16 NC8:8 DUMPI:8 DUMPL:8".split():
+for _n in "RF:1 P32:1 P16:1 PF:1 WC:1 HKF:2 THF:2 NM15:1 K0:1 BA:1 BB:1 EN:1 C4K:8".split():
     PART[_n.split(":")[0]] = _at
     _at += int(_n.split(":")[1])
 SCRATCH["CF"] = ("sbuf", [128, _at], "float32")
-SEMAPHORES = ["sv", "ss", "sp", "sg", "ls", "za1", "za2", "zr"] + ["d%d" % i for i in range(14)]
+SEMAPHORES = ["sv", "ss", "sp", "sg", "ls", "za1", "za2", "zr"] + ["d%d" % i for i in range(16)]
 TWO = ("bfloat16", "float16", "uint16")
-COSTS = [dict(cy=1.0, pe=0.5, ga=1.5, sc=3.0, wake=60.0, same=40.0, dma=2000.0, bw=200.0, rem=2500.0),
-         dict(cy=0.9, pe=0.5, ga=1.15, sc=2.0, wake=110.0, same=60.0, dma=2000.0, bw=250.0, rem=3500.0),
-         dict(cy=1.15, pe=0.6, ga=1.95, sc=5.0, wake=60.0, same=40.0, dma=2200.0, bw=150.0, rem=2000.0)]
+COSTS = [dict(cy=0.85, pe=0.42, ga=1.4, sc=3.0, wake=180.0, same=150.0, fx=40.0, dma=1000.0, bw=450.0, rem=2500.0),
+         dict(cy=0.83, pe=0.42, ga=1.1, sc=2.0, wake=250.0, same=150.0, fx=40.0, dma=1500.0, bw=350.0, rem=3500.0),
+         dict(cy=1.1, pe=0.55, ga=1.9, sc=5.0, wake=150.0, same=120.0, fx=40.0, dma=1500.0, bw=300.0, rem=2000.0)]
 TRIALS = 5000
-GW, GO, YW = "SWWS", (1, 0, 2, 3), "SVVV"
+CFG = dict(G=["S01 W24 S12"] * 3, GS=["01 24 12"] * 3, Y=["W01 S12 W23 S34"] * 3, YS=["01 12 23 34"] * 3, X=["S01 V34 S12 S23"] * 3, L=["02 24"] * 3,
+           M=["02 24"] * 3, ZN="VVV", EI="SSS", EL="SSV", WI="SSS", WL="SSV", TO="VVV", JH="GGG", NE=8)
 ORDER = {}
 
 
@@ -60,8 +60,8 @@ def schedule(ops):
         for j, w in pred[i]: succ[j].append((i, w))
     cost, lat, hop = [], [], []
     for C in COSTS:
-        cost.append([o["f"][0] + C["cy"] * (o["f"][1] + C["ga"] * o["f"][2] + C["sc"] * o["f"][3]) + C["pe"] * o["f"][4] for o in ops])
-        lat.append([o["lat"][0] * C["dma"] + o["lat"][1] / C["bw"] + o["lat"][2] * C["rem"] for o in ops])
+        cost.append([o["f"][0] + C["cy"] * (o["f"][1] + C["ga"] * o["f"][2] + C["sc"] * o["f"][3]) + C["pe"] * o["f"][4] + o["lat"][1] / C["bw"] + C["fx"] * (o["q"] in "VS") for o in ops])
+        lat.append([o["lat"][0] * C["dma"] + o["lat"][2] * C["rem"] for o in ops])
         hop.append((C["wake"], C["same"]))
 
     def length(order, s):
@@ -129,7 +129,7 @@ def schedule(ops):
         if it == 0: base = [length(order, s) for s in range(len(COSTS))]
         e = sum([length(order, s) / base[s] for s in range(len(COSTS))])
         if e < best[0]: best = (e, order, key, look)
-    return length(best[1], 0), best[1]
+    return [length(best[1], s) for s in range(len(COSTS))], best[1]
 
 
 def make(g, T):
@@ -151,7 +151,7 @@ def make(g, T):
                 acc += [(r[1], False), (r[2], False)] if len(r) == 3 else [(r, False)]
         for r in outs:
             acc += [(r[1], True), (r[2], False)] if len(r) == 3 else [(r, True)]
-        pre = {j: True for j in extra}
+        pre = dict(extra)
         for r, w in acc:
             ps = r[0] in PSUM
             h = hist.setdefault(r[0], [])
@@ -171,7 +171,8 @@ def make(g, T):
             elif w and not ps and r[3] == 1:
                 h[:] = [a for a in h if a[0] == i or not (a[1][1] >= r[1] and a[1][2] <= r[2] and a[1][4] >= r[4] and a[1][5] <= r[5])]
             h.append((i, r, w))
-        ops.append(dict(q=q, call=call, f=tuple(f) + (0,) * (5 - len(f)), lat=lat, pre=pre, sem=sem or own.get(q), inc=inc))
+        name = (outs[0][1][0] + "!" if len(outs[0]) == 3 else outs[0][0]) if outs else "-"
+        ops.append(dict(q=q, call=call, f=tuple(f) + (0,) * (5 - len(f)), lat=lat, pre=pre, sem=sem or own.get(q), inc=inc, name=name))
         return i
 
     def sc(x): return ap(x) if isinstance(x, tuple) else x
@@ -197,6 +198,9 @@ def make(g, T):
     def scan(out, a, b, o1, o2):
         add("V", [out], [a, b], lambda n: n.tensor_tensor_scan(ap(out), ap(a), ap(b), 0.0, o1, o2), vcost(out, a, half(out, a, b)))
 
+    def least(out, in_):
+        add("V", [out], [in_], lambda n: n.tensor_reduce(ap(out), ap(in_), AxisListType.X, ALU.min, apply_absolute_value=True), (0, max(64, wid(in_))))
+
     def fill(out, v): add("V", [out], [], lambda n: n.memset(ap(out), v), vcost(out, out, half(out)))
 
     def act(out, in_, f, bias=0.0, scale=1.0, acc=None):
@@ -217,32 +221,35 @@ def make(g, T):
 
     def cast(out, in_): asel(out, in_, [[0, wid(out)]], ALU.is_gt, 0.0, 1, 0)
 
-    nd = [0]
+    nd = [0, None]
 
     def dma(q, out, in_):
         sem = "d%d" % nd[0]
         nd[0] += 1
-        o = T[out][:] if isinstance(out, str) else ap(out)
-        i = T[in_][:] if isinstance(in_, str) else ap(in_)
-        s = in_ if isinstance(out, str) else out
+        load = isinstance(in_, str)
+        o = ap(out) if load else T[out][:]
+        x = T[in_][:] if load else ap(in_)
+        s = out if load else in_
         by = wid(s) * 128 * (2 if kind(s) in TWO else 4)
-        add(q, [] if isinstance(out, str) else [out], [] if isinstance(in_, str) else [in_], lambda n: n.dma_start(o, i), (60,), (1, by, 0), sem, 16)
+        i = add(q, [], [] if load else [in_], lambda n: n.dma_start(o, x), (60,), (0, 0, 0), sem, 16)
+        nd[1] = add("dq", [out] if load else [], [], None, (0,), (1, by, 0), sem, 0, [(i, True)] + ([(nd[1], False)] if load and nd[1] is not None else []))
 
     def send(out, in_, rsem, dst, src, topo):
         rid, pid, _ = topo.addr(dst)
-        en = topo.engines(src, dst)[:8]
+        en = topo.engines(src, dst)[:CFG["NE"]]
         i = add("G", [], [in_], lambda n: n.remote_dma(ap(out), ap(in_), T.sem[rsem], T.sem["ls"], pid, rid, sum(1 << x for x in en)), (1000,), (0, 0, 1), "ls", len(en))
-        add("net", [out], [], None, (0,), (0, 0, 0), rsem, len(en), (i,))
+        add("net", [out], [], None, (0,), (0, 0, 0), rsem, len(en), [(i, True)])
 
     def run():
-        if not ORDER:
+        if "best" not in ORDER:
+            ORDER["ops"] = ops
             ORDER["best"] = schedule(ops)
         cnt, known, tok = {}, {q: {} for q in eng}, {}
         for i in ORDER["best"][1]:
             o = ops[i]
             q = o["q"]
             cnt[o["sem"]] = cnt.get(o["sem"], 0) + o["inc"]
-            if q == "net":
+            if q not in eng:
                 tok[i] = (o["sem"], cnt[o["sem"]], {})
                 continue
             k = known[q]
@@ -260,7 +267,7 @@ def make(g, T):
         for s in sorted(cnt):
             if known["G"].get(s, 0) < cnt[s]: g.wait_ge(T.sem[s], cnt[s])
 
-    return dict(cp=cp, tt=tt, ts=ts, scan=scan, fill=fill, act=act, mm=mm, iota=iota, asel=asel, cast=cast, dma=dma, send=send, run=run)
+    return dict(cp=cp, tt=tt, ts=ts, scan=scan, least=least, fill=fill, act=act, mm=mm, iota=iota, asel=asel, cast=cast, dma=dma, send=send, run=run)
 
 
 def rank_program(g, core, T, topo):
@@ -269,322 +276,311 @@ def rank_program(g, core, T, topo):
         return
     n = len(T.cores)
     m = make(g, T)
-    cp, tt, ts, scan, fill, act, mm, iota, asel, cast, dma = (m[k] for k in ("cp", "tt", "ts", "scan", "fill", "act", "mm", "iota", "asel", "cast", "dma"))
+    cp, tt, ts, scan, least, fill, act, mm, iota, asel, cast, dma = (m[k] for k in ("cp", "tt", "ts", "scan", "least", "fill", "act", "mm", "iota", "asel", "cast", "dma"))
     F = lambda b: R(b, 0, SCRATCH[b][1][1])
     C = lambda b, i=0: R(b, i, i + 1)
     S8 = lambda i: R("WLF", 8 * i, 8 * i + 8)
-    K8 = lambda i: R("KJ", 8 * i, 8 * i + 8)
     D8 = lambda b: R(b, 0, 8)
     G8 = lambda i: R("G8", 8 * i, 8 * i + 8)
-    C8 = G8(2)
-    PU, PP, PQ, PZ = R("p0", 0, 128), R("p0", 128, 256), R("p0", 256, 384), R("p0", 384, 512)
-    KEY, E8, REC8, AA = R("p1", 0, 128), R("p1", 128, 136), R("p1", 136, 144), R("p1", 144, 145)
-    CNT, CNB, JJB = R("p3", 128, 256), R("p3", 256, 384), R("p3", 384, 512)
-    ST, FT = R("p4", 128, 256), R("p4", 256, 384)
-    J8, CN8 = R("p7", 96, 104), R("p7", 104, 112)
-    HP, DP, JNP = R("p7", 128, 256), R("p7", 256, 384), R("p7", 384, 512)
-    WI, WL, WX, WG = F("IX"), F("LK"), F("XC"), F("GI")
+    END = lambda b: R(b, 15, 128, 16)
+    C8, REP, LAST = G8(0), R("OFFG", 0, 8), R("OFFG", 8, 16)
+    WEIGHT = {32768: G8(1), -32768: G8(2), 65536: G8(3), -65536: G8(4), 1: G8(0)}
+    PU, PU2, PE, AA = R("p0", 0, 128), R("p0", 128, 256), R("p0", 256, 384), R("p0", 128, 129)
+    PT, PV = R("p6", 0, 128), R("p6", 128, 256)
+    KEY, E8, GD8 = R("p1", 0, 128), R("p1", 128, 136), R("p1", 136, 144)
+    PZ, J8, PLA = R("p3", 128, 256), R("p3", 64, 72), R("p3", 384, 512)
+    FT, PNA = R("p4", 128, 256), R("p4", 256, 512)
+    WI, WL, WX, WG = R("IX", 128, 1152), R("LK", 128, 2176), F("XC"), R("GI", 128, 1152)
+    IDB, SHB, NIDB, P4K, N4K, ONES = R("IDB", 0, 128), R("IDB", 1, 129), F("NIDB"), F("P4K"), F("N4K"), F("ONESB")
+    plan = lambda k, t: [(p[:-2], int(p[-2]), int(p[-1])) for p in CFG[k][t].split()]
 
-    dma("Y", F("Z0"), "zc"); dma("Y", F("WTI"), "wt"); dma("Y", F("HKI"), "hk")
-    dma("S", R("GI", 0, 1024), "gi"); dma("Y", F("IXI"), "ix"); dma("Y", F("THI"), "th"); dma("S", F("XC"), "xc"); dma("Y", F("LKI"), "lk")
+    dma("Y", F("WTI"), "wt"); dma("Y", F("Z0"), "zc"); dma("Y", F("HKI"), "hk")
+    dma("S", WG, "gi"); dma("Y", F("IXI"), "ix"); dma("Y", F("THI"), "th"); dma("S", F("XC"), "xc"); dma("Y", F("LKI"), "lk")
 
-    fill(F("ONES"), 1.0)
-    iota(F("PIO"), [[0, 16]], 0, 1)
-    asel(F("IDF"), F("ONES"), [[-1, 128]], ALU.is_equal, 0.0, 0, 1)
-    asel(F("BOF"), F("ONES"), [[-16, 8], [0, 16]], ALU.is_ge, 0.0, 0, 1)
-    asel(F("BOF"), F("BOF"), [[16, 8], [0, 16]], ALU.is_ge, 0.0, 15, -1)
+    iota(F("PIO"), [[0, 1]], 0, 1)
+    iota(F("HQ"), [[16, 8], [0, 16]], 0, 0)
+    iota(F("DIF"), [[1, 144]], 0, -1)
     iota(F("RQ"), [[0, 8], [1, 16]], 0, 0)
-    iota(F("CIO"), [[1, 8]], 0, 0)
-    asel(F("SHF"), F("ONES"), [[-1, 128]], ALU.is_equal, 0.0, -1, 1)
-    asel(F("UT"), F("BOF"), [[1, 128]], ALU.is_ge, 0.0, 0, -1)
-    fill(R("ZS", 512, 1536), 0.0)
-    for h in (0, 1):
-        fill(R("RX", 1024 * h, 1024 * h + 1024), 1.0)
-    fill(R("RX", 0, 2048, 16), 0.0)
-    fill(F("ONESB"), 1.0)
-    fill(F("EB"), 0.0)
-    for q in (0, 3, 1, 2):
-        asel(R("RM", 512 * q, 512 * q + 512), F("ONESB"), [[-1, 32], [0, 16]], ALU.is_equal, 0.0, -32 * q, 1)
-    for c in range(8):
-        act(R("R1", SEG[c], SEG[c + 1]), R("IDF", 0, 16 * c + 16), ACT.Copy)
-    ts(F("PR"), F("PIO"), 15, ALU.bitwise_and)
-    act(F("BOB"), F("BOF"), ACT.Copy)
-    cp(C("RF"), C("PR"))
-    act(F("IDB"), F("IDF"), ACT.Copy)
-    act(F("NIDB"), F("IDF"), ACT.Copy, scale=-1.0)
+    iota(F("J32"), [[1, 32], [0, 16]], 0, 0)
+    iota(R("CIO", 0, 8), [[1, 8]], 0, 0)
+    iota(R("CIO", 8, 16), [[16, 8]], 15, 0)
+    iota(R("CIO", 16, 32), [[16, 16]], 0, 0)
+    iota(C("PF"), [[0, 1]], -2048, 1)
+    for i, v in enumerate((15, 31, 112)):
+        ts(C("PR", i), F("PIO"), v, ALU.bitwise_and)
+    cp(R("RF", 0, 3), F("PR"))
+    ts(F("BOB"), F("HQ"), C("P16"), ALU.is_equal)
+    ts(F("IDB"), F("DIF"), 0.0, ALU.is_equal)
+    for b, v in (("N4K", -4096), ("IDF", 1), ("NIDB", -1), ("P4K", 4096), ("HID", 255 / 512)):
+        act(F(b), IDB, ACT.Copy, scale=float(v))
+    fill(ONES, 1.0)
     cp(C("WC"), C("WTI"))
-    ts(F("WB"), F("BOF"), C("WC"), ALU.mult)
-    cp(R("HKF", 0, 2), F("HKI"))
-    ts(F("PD"), F("IDF"), C("HKF", 0), ALU.mult)
-    ts(F("QD"), F("IDF"), C("HKF", 1), ALU.mult)
-    PA, PB = R("p1", 128, 256), R("p1", 256, 384)
-    mm((PA, F("BOB"), F("PD"), True, True), (PB, F("BOB"), F("QD"), True, True))
-    ts(F("PWI"), PA, C("WC"), ALU.mult)
-    ts(F("QWI"), PB, C("WC"), ALU.mult)
-    ts(F("PWI"), F("PWI"), 1023, ALU.bitwise_and)
-    ts(F("QWI"), F("QWI"), 2047, ALU.bitwise_and)
-    cp(F("PW"), F("PWI"))
-    cp(F("QW"), F("QWI"))
+    ts(F("WB"), F("BOB"), C("WC"), ALU.mult)
+    ts(C("HKF", 0), C("HKI", 0), 2.0, ALU.mult, -1792.0, ALU.add)
+    ts(C("HKF", 1), C("HKI", 1), -1792.0, ALU.add)
+    for d, w, wi, i, P in (("PD", "PW", "PWI", 0, R("p1", 128, 256)), ("QD", "QW", "QWI", 1, R("p3", 128, 256))):
+        ts(F(d), IDB, C("HKF", i), ALU.mult)
+        mm((P, F("BOB"), F(d), True, True))
+        ts(F(wi), P, C("WC"), ALU.mult)
+        ts(F(wi), F(wi), 2047, ALU.bitwise_and)
+        ts(F(w), F(wi), 16.0, ALU.mult)
+    ts(F("RM"), F("J32"), C("P32"), ALU.is_equal)
     ts(F("M16"), F("RQ"), C("RF"), ALU.is_equal)
-    ts(F("RMIN"), F("RQ"), 0.0, ALU.is_equal, 3.0e7, ALU.mult)
-    ts(F("RMAX"), F("RMIN"), -2.0, ALU.mult, 3.0e7, ALU.add)
-    for i, v in enumerate((16384.0, 32768.0, 1.0, -0.5, None, -16384.0, 65536.0, -32768.0)):
-        if v is not None: act(G8(i), R("BOF", 0, 128, 16), ACT.Copy, scale=v)
-    cp(F("OFFG"), F("CIO"))
-    act(F("MROW"), F("RQ"), ACT.Copy, scale=1024.0)
-    ts(C("JJC"), C("RF"), -2048.0, ALU.mult, 30720.0, ALU.add)
-    fill(R("IX", 1024, 1152), 0.0)
-    fill(R("LK", 2048, 2192), 0.0)
-    fill(R("GI", 1024, 1152), 0.0)
-    fill(R("XG", 2048, 2064), 0.0)
-    act(F("M16B"), F("M16"), ACT.Copy)
-    for k in range(0, 16, 4):
-        asel(R("SEL", 128 * k, 128 * k + 512), F("ONESB"), [[-1, 4], [-1024, 8], [-63, 16]], ALU.is_equal, 0.0, -k, 64)
-    for at, v in ((0, 1.0), (144, 2.0), (288, -1.0)):
-        act(R("EB", at + 15, at + 143, 16), R("BOF", 0, 128, 16), ACT.Copy, scale=v)
-    ts(D8("NC8"), R("BOF", 0, 128, 16), -1.0, ALU.mult)
+    act(R("MK", 0, 128), F("M16"), ACT.Copy)
+    for a in (128, 256, 512):
+        act(R("MK", a, 2 * a), R("MK", 0, a), ACT.Copy)
+    fill(F("RX"), 1.0)
+    fill(R("RX", 0, 1024, 16), 0.0)
+    act(F("RS"), R("RX", 0, 128), ACT.Copy, scale=-67108864.0, bias=33554432.0)
+    act(F("RC"), R("RX", 0, 128), ACT.Copy, scale=73.5, bias=-9.5)
+    act(F("TH16"), F("M16"), ACT.Copy, scale=99.0, bias=-99.0)
+    act(R("CRI", 0, 128, 1, 0, 64), R("RQ", 0, 128, 1, 0, 64), ACT.Copy, scale=32.0, bias=16.0)
+    fill(R("CRI", 0, 128, 1, 64, 128), -262144.0)
+    act(R("CRL", 0, 128, 1, 0, 64), R("RQ", 0, 128, 1, 0, 64), ACT.Copy, scale=32.0, bias=-512.0)
+    fill(R("CRL", 0, 128, 1, 64, 128), 262144.0)
+    for v, r in WEIGHT.items():
+        act(r, R("BOB", 0, 128, 16), ACT.Copy, scale=float(v))
+    for i, v in ((5, -896), (6, 127), (7, 2048)):
+        iota(G8(i), [[0, 8]], v, 0)
+    cp(F("OFFG"), R("CIO", 0, 16))
+    for a, b in sorted(set((a, b) for t in range(RO) for w, a, b in plan("G", t) if w != "S")):
+        fill(R("ZS", 512 * a, 512 * b), 0.0)
+    for b in ("IX", "LK", "GI"):
+        iota(R(b, 0, 128), [[0, 128]], 0, 0)
+    iota(R("XG", 2048, 2064), [[0, 16]], 0, 0)
+    iota(R("STEP", 0, 16), [[0, 16]], 1, 0)
+    iota(F("W16"), [[0, 128]], 16, 0)
+    act(F("UT"), R("DIF", 0, 128), ACT.Sign, bias=0.5)
+    act(D8("C4K"), C8, ACT.Copy, scale=4096.0)
+    iota(F("RD"), [[0, 576]], 0, 0)
     for c in range(8):
-        act(R("R2", SEG[c], SEG[c + 1]), R("ONESB", 0, 16 * c + 16), ACT.Copy, scale=C("NC8", c))
-    fill(F("R3"), 0.0)
-    for c in range(8):
-        act(R("R3", SEG[c + 1] - 16, SEG[c + 1]), R("UT", 16 * c, 16 * c + 16), ACT.Copy, scale=4096.0)
-    fill(F("RD"), 0.0)
-    for c in range(8):
-        fill(C("RD", SEG[c]), 1.0e6)
-    ts(C("ENDF", 0), C("RF"), 7.0, ALU.min)
-    ts(C("ENDF", 1), C("ENDF", 0), 8.0, ALU.mult, 24.0, ALU.add)
-    tt(C("ENDF", 2), C("ENDF", 0), C("ENDF", 1), ALU.mult)
-    ts(C("ENDS"), C("ENDF", 2), 15.0, ALU.add)
-    ts(D8("DUMPI"), F("CIO"), 16.0, ALU.mult, C("RF"), ALU.add)
-    ts(D8("DUMPL"), D8("DUMPI"), 2049.0, ALU.add)
-    ts(D8("DUMPI"), D8("DUMPI"), 1024.0, ALU.add)
-    ts(F("MNEG"), F("M16"), 128.0, ALU.mult, -128.0, ALU.add)
-    cp(R("THF", 0, 2), F("THI"))
+        cast(R("R1", SEG[c], SEG[c + 1]), R("P4K", 0, 16 * c + 16))
+        act(R("R2", SEG[c], SEG[c + 1]), R("UT", 0, 16 * c + 16), ACT.Copy, scale=C("C4K", c))
+        iota(C("RD", SEG[c]), [[0, 1]], 1 << 20, 0)
+    act(C("EN"), C("RF"), ACT.Square, bias=1.5)
+    ts(C("EN"), C("EN"), 8.0, ALU.mult, -3.0, ALU.add)
+    ts(C("ENDS"), C("EN"), 575.0, ALU.min)
+    ts(F("DUMP"), R("CIO", 16, 32), C("RF"), ALU.add)
+    ts(F("DL"), C8, C("PF"), ALU.mult)
+    ts(C("K0"), C("RF"), 0.0, ALU.is_equal, 4096.0, ALU.mult)
+    act(C("BA"), C("K0"), ACT.Copy, scale=-1.0)
+    act(C("BB"), C("K0"), ACT.Copy, bias=-4096.0)
     ts(C("NM15"), C("RF"), 15.0, ALU.is_equal, 2000.0, ALU.mult)
-    tt(C("ACOL"), C("THF", 0), C("NM15"), ALU.subtract)
-    ts(C("BCOL"), C("THF", 1), -1.0, ALU.mult, 1023.5, ALU.add)
-    act(F("HID"), F("IDF"), ACT.Copy, scale=0.5)
-    act(F("NHID"), F("IDF"), ACT.Copy, scale=-0.5)
-    act(F("IDK"), F("IDF"), ACT.Copy, scale=512.0)
-    act(F("NID4K"), F("IDF"), ACT.Copy, scale=-4096.0)
-    act(F("SHB"), F("SHF"), ACT.Copy)
-    fill(G8(4), -7.0)
-    fill(F("M24"), -16777216.0)
-    fill(F("HALF"), 0.5)
-    fill(C("M95"), -9.5)
+    tt(C("THF", 0), C("THI", 0), C("NM15"), ALU.subtract)
+    ts(C("THF", 1), C("THI", 1), -1.0, ALU.mult)
+    ts(F("TD"), IDB, C("THF", 0), ALU.mult)
+    ts(F("TB"), IDB, C("THF", 1), ALU.mult)
+    mm((FT, ONES, F("TD"), True, True))
+    act(F("THR"), FT, ACT.Copy, bias=16744448.0, scale=-32768.0)
     for h in (0, 512):
-        cast(R("IX", h, h + 512), R("IXI", h, h + 512))
+        cast(R("IX", h + 128, h + 640), R("IXI", h, h + 512))
 
     def ustage(t):
         z = F("Z%d" % t)
-        if t: mm((PU, F("WB"), z, True, True), (PP, F("PW"), z, True, True), (PQ, F("QW"), z, True, True))
-        else: mm((PU, F("WB"), z, True, True))
-        cp(F("UI"), PU)
-        if not t: mm((PP, F("PW"), z, True, True))
-        if not t: mm((PQ, F("QW"), z, True, True))
-        ts(F("UI"), F("UI"), 4095, ALU.bitwise_and)
-        tt(F("UU"), F("UI"), F("UI"), ALU.mult)
-        ts(F("S5"), F("UU"), 5, ALU.arith_shift_right, 1023, ALU.bitwise_and)
-        tt(F("BS"), PP, F("S5"), ALU.add)
-        ts(F("VQ"), F("UU"), 4, ALU.arith_shift_right, 2047, ALU.bitwise_and)
-        tt(F("VQ"), PQ, F("VQ"), ALU.add)
-        ts(F("VQ"), F("VQ"), 2047, ALU.bitwise_and)
-        cp(F("VH"), F("VQ"))
-        cp(R("ZS", 512, 1536, 16), R("Z%d" % t, 32, 96))
-        scan(R("ZREP", 512, 1536), R("RX", 512, 1536), R("ZS", 512, 1536), ALU.mult, ALU.add)
-        mm((R("p0", 384, 512), z, F("NIDB"), True, True))
-        act(F("ZT%d" % (t & 1)), R("p0", 384, 512), ACT.Copy)
+        mm((PU, F("WB"), z, True, True))
+        act(F("QB"), PU, ACT.Copy, bias=191.5, scale=1 / 4096)
+        mm((PU2, F("WB"), z, True, False), (PU2, N4K, F("QB"), False, True))
+        act(F("UU"), PU2, ACT.Square, bias=784384.0)
+        if t: mm((PE, F("PW"), z, True, False), (PE, F("IDF"), F("UU"), False, True))
+        else:
+            mm((PE, F("PW"), z, True, True))
+            estage(0)
+        mm((PT, z, NIDB, True, True))
+        act(F("ZT%d" % (t & 1)), PT, ACT.Copy)
+        mm((PV, F("QW"), z, True, True))
+        tt(F("VI"), PV, F("UU"), ALU.add)
+        ts(F("VI"), F("VI"), 4, ALU.arith_shift_right, 2047, ALU.bitwise_and)
+        cast(F("VH%d" % (t & 1)), F("VI"))
+        for w, a, b in plan("G", t):
+            if w != "S":
+                cp(R("ZS", 512 * a, 512 * b, 16), R("Z%d" % t, 32 * a, 32 * b))
+                scan(R("ZREP", 512 * a, 512 * b), R("RX", 0, 512 * (b - a)), R("ZS", 512 * a, 512 * b), ALU.mult, ALU.add)
 
     def estage(t):
-        b = F("BS")
-        if t:
-            ts(F("EI"), b, AA, ALU.add, 8192.0, ALU.add)
-            b = F("EI")
-        ts(F("EM"), b, 1023, ALU.bitwise_and)
-        cp(F("EU"), F("EM"))
-        cast(F("MKEY"), F("EM"))
-        mm((KEY, F("MKEY"), F("IDF"), True, False))
+        if t: ts(F("EI"), PE, AA, ALU.add, 16384.0, ALU.add)
+        else: tt(F("EI"), PE, F("UU"), ALU.add)
+        ts(F("EI"), F("EI"), 5, ALU.arith_shift_right, 1023, ALU.bitwise_and)
+        cp(F("EU"), F("EI"))
+        cast(F("EH"), F("EI"))
 
-    def zsub(p, t, a, b): return (p, F("ZT%d" % (t & 1)), R("RM", a, b), True, False)
+    def zsub(p, t, q): return (p, R("ZT%d" % (t & 1), 0, 128, 1, 32 * q, 32 * q + 32), R("RM", 0, 512, 1, 32 * q, 32 * q + 32), True, False)
 
-    def dist(win, off, sub, sh, who, t=None):
-        bank = ["p2", "p5" if sub == "ZREP" else "p6"]
+    def dist(win, off, sub, sh, pieces, t=None):
         DG, AG = ("DG", "AG") if sub == "ZREP" else ("DY", "AY")
-        for q in range(4):
-            a, b = 512 * q, 512 * q + 512
-            if who[q] == "S":
-                p = bank.pop(0)
-                x = 512 * (p != "p2")
-                act(R("GR", x, x + 512), ind(win, R(off, 32 * q, 32 * q + 32)), ACT.Copy)
-                P = R(p, 0, 512)
-                if sub == "ZREP": mm(zsub(P, t, a, b))
-                else: mm((P, F("NIDB"), R(sub, a + sh, b + sh), True, False))
-                mm((P, F("IDB"), R("GR", x, x + 512), False, True))
-                act(R(AG, a, b), R(p, 0, 512), ACT.Abs)
+        x = 0
+        for (who, q, e) in pieces:
+            a, b = 512 * q, 512 * e
+            lst = ind(win, R(off, 32 * q, 32 * e))
+            if who == "S":
+                P, raw = R(("p2", "p5")[x], 0, 512), R("GR", 512 * x, 512 * x + 512)
+                x = 1 - x
+                act(raw, lst, ACT.Copy)
+                mm(zsub(P, t, q) if sub == "ZREP" else (P, NIDB, R(sub, a + sh, b + sh), True, False))
+                mm((P, IDB, raw, False, True))
+                act(R(AG, a, b), P, ACT.Abs)
             else:
-                tt(R(DG, a, b), ind(win, R(off, 32 * q, 32 * q + 32)), R(sub, a + sh, b + sh), ALU.subtract)
-                if who[q] == "V": act(R(AG, a, b), R(DG, a, b), ACT.Abs)
+                tt(R(DG, a, b), lst, R(sub, a + sh, b + sh), ALU.subtract)
+                if who == "V": act(R(AG, a, b), R(DG, a, b), ACT.Abs)
                 else: ts(R(AG, a, b), R(DG, a, b), 0.0, ALU.max)
 
-    def runs(who):
-        out = []
-        for q in range(4):
-            w = who[q] == "W"
-            if q % 2 and out[-1][2] == w: out[-1] = (out[-1][0], q + 1, w)
-            else: out.append((q, q + 1, w))
-        return out
+    def lanesum(out, x, a, b, pos, ks, w):
+        for (buf, wt) in ((("D" + x, -w), ("A" + x, 2 * w)) if pos else (("A" + x, w),)):
+            mm(*[(R(out[0], out[1] + k, out[1] + 128, 16, 32 * a, 32 * b), R(buf, 512 * a + k, 512 * b, 16), WEIGHT[wt], False, False) for k in range(ks)])
 
-    def lanesum(out, who, pieces, ks, one, two, neg):
-        for (a, b, w) in pieces:
-            x = "G" if out[0] == "p1" else "Y"
-            for (buf, wt) in ((("D" + x, neg), ("A" + x, two)) if w else (("A" + x, one),)):
-                mm(*[(R(out[0], out[1] + k, out[1] + 128, 16, 32 * a, 32 * b), R(buf, 512 * a + k, 512 * b, 16), wt, False, False) for k in ks])
+    def sums(out, x, t, ks, w):
+        for (_, a, b) in plan(x + "S", t):
+            lanesum(out, x, a, b, any(who == "W" and q <= a < e for who, q, e in plan(x, t)), ks, w)
 
     def gstage(t):
-        dist(WG, "EU", "ZREP", 0, GW, t)
-        for q in GO:
-            lanesum(("p1", 0), GW, [(q, q + 1, GW[q] == "W")], range(16), G8(0), G8(1), G8(5))
-        mm((KEY, F("IDB"), F("MROW"), False, True))
+        mm((KEY, ONES, F("CRI"), True, False))
+        dist(WG, "EU", "ZREP", 0, plan("G", t), t)
+        sums(KEY, "G", t, 16, 32768)
+        mm((KEY, F("EH"), IDB, False, True))
 
     def argstage(t):
-        scan(F("KMIN"), F("RMIN"), KEY, ALU.max, ALU.min)
-        ts(F("KA"), R("KMIN", 15, 128, 16), 1023, ALU.bitwise_and)
-        tt(F("ERM"), ind(F("KA"), F("OFFG")), F("M16"), ALU.mult)
-        mm((E8, F("ERM"), C8, True, True))
-        cp(F("E8U"), E8)
+        scan(F("KMIN"), F("RS"), KEY, ALU.max, ALU.min)
+        ts(F("KA"), END("KMIN"), 2047, ALU.bitwise_and)
+        tt(F("ERM"), ind(F("KA"), REP), F("M16"), ALU.mult)
+        mm((E8, IDB, G8(5), True, False), (E8, F("ERM"), C8, False, True))
+        ts(F("E8U"), E8, -128.0, ALU.add)
         cp(F("JU"), ind(F("IXI") if t == 0 else WI, F("E8U")))
-        act(F("JJ%d" % (t & 1)), ind(WI, F("E8U")), ACT.Identity, bias=C("JJC"))
-        cp(F("JH"), F("JU"))
+        (cast if CFG["JH"][t] == "G" else cp)(F("JH%d" % (t & 1)), F("JU"))
 
     def lkx(t):
         lk = F("LKI") if t == 0 else WL
+        for (_, a, b) in plan("L", t):
+            tt(R("LG", 512 * a, 512 * b), ind(lk, R("JU", 32 * a, 32 * b)), R("MK", 0, 512 * (b - a)), ALU.mult)
         for h in (0, 1):
-            L = 1024 * h
-            cp(R("LG", L, L + 1024), ind(lk, R("JU", 64 * h, 64 * h + 64)))
             p = R(("p3", "p4")[h], 0, 64)
-            mm(*[(p, R("SEL", 128 * k, 128 * k + 128), R("LG", L + k, L + 1024, 16), k == 0, k == 15) for k in range(16)])
+            mm(*[(p, IDB, R("LG", 1024 * h + k, 1024 * h + 1024, 16), k == 0, k == 15) for k in range(16)])
             cp(R("NU", 64 * h, 64 * h + 64), p)
-        for q in range(4):
-            act(R("XG", 512 * q, 512 * q + 512), ind(WX, R("JU", 32 * q, 32 * q + 32)), ACT.Copy)
+        for (w, a, b) in plan("X", t):
+            o, lst = R("XG", 512 * a, 512 * b), ind(WX, R("JU", 32 * a, 32 * b))
+            if w == "S": act(o, lst, ACT.Copy)
+            else: cp(o, lst)
 
-    def pairs(masked, plain):
-        for (a, b, P) in ((0, 512, R("p6", 0, 512)), (512, 576, R("p7", 0, 64))):
-            mm((P, F("M16B"), R("R3", a, b), True, False), (P, F(plain), R("R1", a, b), False, False), (P, F(masked), R("R2", a, b), False, True))
-            act(R("XA", a, b), P, ACT.Abs)
-
-    def lost(out16):
-        scan(F("XS"), F("RD"), F("XA"), ALU.max, ALU.min)
-        ts(out16, ind(F("XS"), C("ENDS")), 0.0, ALU.is_le)
+    def pairs(masked, plain, bank, who, x):
+        for (a, b, P) in ((0, 448, R("p6", 0, 448)), (448, 576, R(bank, 256, 384))):
+            mm((P, F(plain), R("R1", a, b), True, False), (P, F(masked), R("R2", a, b), False, True))
+            if who == "S": act(R("XA", a, b), P, ACT.Abs)
+        if who == "S":
+            scan(F("XS"), F("RD"), F("XA"), ALU.max, ALU.min)
+            tt(R("TW", x, x + 16), ind(F("XS"), C("ENDS")), F("DUMP"), ALU.add)
+        else:
+            for c in range(8):
+                least(C("TW", x + 8 + c), R("p6", SEG[c], SEG[c + 1]) if c < 7 else R(bank, 256, 384))
+            tt(R("TW", x, x + 8), R("TW", x + 8, x + 16), D8("DUMP"), ALU.add)
+        return R("TW", x, x + 8)
 
     def idx(t):
-        cp(F("ERU"), ind(F("KA"), F("OFFG")))
-        pairs("ERM", "ERU")
-        lost(R("WLF", 16, 32))
-        tt(S8(0), S8(2), D8("DUMPI"), ALU.mult)
-        tt(S8(0), E8, S8(0), ALU.max)
-        cp(F("NOFF"), S8(0))
+        if CFG["EI"][t] == "V": cp(F("ERU"), ind(F("KA"), REP))
+        else:
+            cast(S8(7), F("KA"))
+            act(F("ERF"), ind(S8(7), REP), ACT.Copy)
+            cast(F("ERU"), F("ERF"))
+        w = pairs("ERM", "ERU", "p1", CFG["WI"][t], 0)
+        if t < RO - 1:
+            tt(S8(1), E8, w, ALU.min)
+            cp(F("NOFF"), S8(1))
+        else: tt(F("NOFF"), E8, w, ALU.min)
 
     def znext(t):
-        for h in (0, 1024):
-            scan(R("XM", h, h + 1024), R("RX", h, h + 1024), R("XG", h, h + 1024), ALU.mult, ALU.max)
-        mm((PZ, F("IDB"), F("Z%d" % t), True, False), (PZ, F("IDB"), R("XM", 15, 2048, 16), False, True))
-        act(F("ZH"), PZ, ACT.Copy, bias=129.75, scale=0.5)
-        act(F("ZN%d" % t), F("ZH"), ACT.Copy, bias=-130.0)
+        for (_, a, b) in plan("M", t):
+            scan(R("XM", 512 * a, 512 * b), R("RX", 0, 512 * (b - a)), R("XG", 512 * a, 512 * b), ALU.mult, ALU.max)
+        mm((PU, F("HID"), F("Z%d" % t), True, False), (PU, F("HID"), R("XM", 15, 2048, 16), False, True))
+        if CFG["ZN"][t] == "V": ts(F("ZN%d" % t), PU, 12582912.0, ALU.add, -12582912.0, ALU.add)
+        else:
+            act(F("ZH"), PU, ACT.Copy, bias=130.0)
+            act(F("ZN%d" % t), F("ZH"), ACT.Copy, bias=-130.0)
         if t < RO - 1:
             m["send"](F("Z%d" % (t + 1)), F("ZN%d" % t), "za%d" % (t + 1), T.cores[(rank + 1) % n], core, topo)
         else:
             m["send"](F("ZR"), F("ZN%d" % t), "zr", T.cores[(rank - t) % n], core, topo)
 
     def far(t):
-        P = R("p5", 0, 512)
+        P = R("p7", 0, 512)
         for q in range(4):
             a, b = 512 * q, 512 * q + 512
-            mm(zsub(P, t, a, b), (P, F("IDB"), R("XG", a, b), False, True))
+            mm(zsub(P, t, q), (P, IDB, R("XG", a, b), False, True))
             act(R("AF", a, b), P, ACT.Abs)
 
     def ystage(t):
-        dist(WX, "NU", "XG", 1, YW)
-        for (a, b, w) in runs(YW):
-            o = R("p4", 128 + 32 * a, 128 + 32 * b)
-            src = (("DY", 288), ("AY", 144)) if w else (("AY", 0),)
-            for i, (buf, at) in enumerate(src):
-                mm(*[(o, R("EB", at + 15 - k, at + 143 - k), R(buf, 512 * a + k, 512 * b, 16), i == 0 and k == 0, i == len(src) - 1 and k == 14) for k in range(15)])
+        mm((PZ, ONES, F("CRL"), True, False))
+        dist(WX, "NU", "XG", 1, plan("Y", t))
+        sums(PZ, "Y", t, 15, -32768)
+        mm((PZ, F("JH%d" % (t & 1)), IDB, False, True))
 
     def rec(t):
-        ts(F("CMP"), ST, C("ACOL"), ALU.is_le)
-        if t < RO - 1:
-            mm((CNT, F("IDB"), F("MNEG"), True, False), (CNT, F("CMP"), F("BOB"), False, True))
-            act(F("RECS"), CNT, ACT.Sign, bias=C("M95"), acc=F("ACC"))
-            mm((REC8, F("IDB"), G8(4), True, False), (REC8, F("RECS"), G8(3), False, True), (AA, F("HALF"), F("ACC"), True, True))
-        mm((CN8, F("CMP"), C8, True, True))
-        mm((CNB, F("BOB"), F("CMP"), True, True))
+        tt(F("CMP"), PZ, F("THR"), ALU.is_ge)
+        scan(F("KMX"), F("RS"), PZ, ALU.max, ALU.min)
+        scan(F("CNS"), F("RC"), F("CMP"), ALU.min, ALU.add)
+        act(F("RS8"), END("CNS"), ACT.Sign, acc=F("ACC") if t < RO - 1 else None)
+        tt(F("NRM"), ind(F("CNS"), LAST), F("TH16"), ALU.is_lt)
 
     def gists(t):
-        tt(S8(4), REC8, D8("DUMPI"), ALU.mult)
-        tt(F("GOFF"), S8(4), S8(0), ALU.max)
-        cp(ind(WG, F("GOFF")), F("Z%d" % t))
+        mm((GD8, IDB, G8(7), True, False), (GD8, F("NRM"), F("DL"), False, True))
+        tt(F("GOFF"), GD8, S8(1), ALU.min)
+        cp(ind(F("GI"), F("GOFF")), F("Z%d" % t))
 
     def names(t):
-        mm((HP, F("HID"), F("VH"), True, False), (HP, F("HID"), F("JH"), False, True), (DP, F("HID"), F("VH"), True, False), (DP, F("NHID"), F("JH"), False, True))
-        act(F("HV"), HP, ACT.Copy)
-        act(F("RBS"), CNB, ACT.Sign, bias=C("M95"))
-        mm((FT, F("IDK"), F("RBS"), True, False))
-        for h in (0, 1):
-            mm(*[(R("p4", 256 + 64 * h, 320 + 64 * h), R("EB", 15 - k, 143 - k), R("AF", 1024 * h + k, 1024 * h + 1024, 16), False, False) for k in range(16)])
-        mm((FT, F("IDK"), F("RBS"), False, True))
-        act(F("SG"), FT, ACT.Sign, bias=C("BCOL"))
-        tt(F("NT"), DP, F("SG"), ALU.mult)
-        tt(ind(WI, F("NOFF")), F("HV"), F("NT"), ALU.add)
+        mm((FT, ONES, F("TB"), True, False))
+        lanesum(FT, "F", 0, 4, False, 16, 1)
+        mm(*[(R("p4", 128 + k, 256, 16), P4K, F("RS8"), False, k == 15) for k in range(16)])
+        act(F("SG"), FT, ACT.Sign, bias=4095.5)
+        a, b = R("p4", 256, 384), R("p4", 384, 512)
+        mm((a, IDB, F("VH%d" % (t & 1)), True, False), (a, F("SG"), P4K, False, True), (b, IDB, F("JH%d" % (t & 1)), True, False), (b, F("SG"), N4K, False, True))
+        act(F("NA"), PNA, ACT.Copy, bias=-4096.0)
+        tt(ind(F("IX"), F("NOFF")), R("NA", 0, 128), R("NA", 128, 256), ALU.max)
 
     def links(t):
-        JJ = F("JJ%d" % (t & 1))
-        mm((PZ, F("IDB"), F("M24"), True, False))
-        lanesum(("p0", 384), YW, runs(YW), range(15), G8(1), G8(6), G8(7))
-        mm((PZ, JJ, F("IDF"), False, True))
-        scan(F("KMX"), F("RMAX"), PZ, ALU.min, ALU.max)
-        ts(K8(0), R("KMX", 15, 128, 16), 32767, ALU.bitwise_and)
-        ts(K8(1), R("KMX", 15, 128, 16), 2047, ALU.bitwise_and)
-        ts(S8(5), CN8, 10.0, ALU.is_ge, 2048.0, ALU.mult)
-        tt(K8(2), K8(1), S8(5), ALU.max)
-        cast(S8(7), K8(0))
-        act(F("REP2"), ind(S8(7), F("OFFG")), ACT.Copy)
-        mm((JJB, F("REP2"), F("IDF"), True, True))
-        tt(F("ERM2"), ind(K8(2), F("OFFG")), F("M16"), ALU.mult)
-        mm((J8, F("ERM2"), C8, True, True))
-        cp(F("ERU2"), ind(K8(2), F("OFFG")))
-        pairs("ERM2", "ERU2")
-        tt(F("NOH"), JJB, JJ, ALU.not_equal)
-        act(F("NOHB"), F("NOH"), ACT.Copy)
-        mm((JNP, F("SHB"), F("JH"), True, False), (JNP, F("NID4K"), F("NOHB"), False, True))
-        act(F("JN"), JNP, ACT.Copy)
-        cp(F("JX8"), J8)
-        tt(F("TOLD"), ind(WL, F("JX8")), F("NOH"), ALU.mult)
-        lost(R("WLF", 16, 32))
-        tt(S8(6), S8(2), D8("DUMPL"), ALU.mult)
-        tt(F("LOFF"), J8, S8(6), ALU.max)
-        tt(ind(WL, F("LOFF")), F("TOLD"), F("JN"), ALU.max)
+        ts(F("KJ"), END("KMX"), 2047, ALU.bitwise_and)
+        act(S8(2), F("RS8"), ACT.Copy, scale=-2048.5, bias=-2047.5)
+        tt(S8(3), F("KJ"), S8(2), ALU.add)
+        tt(F("ERM2"), ind(S8(3), REP), F("NRM"), ALU.mult)
+        if CFG["EL"][t] == "V": ts(F("ERU2"), ind(S8(3), REP), 0.0, ALU.max)
+        else:
+            act(F("ERF2"), ind(S8(3), REP), ACT.Relu)
+            cast(F("ERU2"), F("ERF2"))
+        cast(F("KE"), END("KMX"))
+        tt(R("STEP", 16, 144), ind(R("KE", 0, 8), REP), F("KMX"), ALU.is_equal)
+        now, was = R("STEP", 16, 144), R("STEP", 15, 143)
+        mm((J8, IDB, G8(6), True, False), (J8, F("ERM2"), C8, False, True))
+        ts(F("JX8"), J8, -128.0, ALU.add)
+        mm((PZ, SHB, F("JH%d" % (t & 1)), True, False), (PZ, now, P4K, False, False), (PZ, was, N4K, False, True))
+        act(R("LA", 128, 256), PZ, ACT.Identity, bias=C("BB"))
+        if CFG["TO"][t] == "V":
+            mm((PLA, now, N4K, True, False), (PLA, was, P4K, False, True))
+            act(R("LA", 0, 128), PLA, ACT.Identity, bias=C("BA"))
+            tt(F("TOLD"), ind(WL, F("JX8")), R("LA", 0, 128), ALU.add)
+        else:
+            act(R("LA", 0, 128), ind(WL, F("JX8")), ACT.Copy)
+            mm((PLA, now, N4K, True, False), (PLA, was, P4K, False, False), (PLA, F("IDF"), R("LA", 0, 128), False, True))
+            act(F("TOLD"), PLA, ACT.Identity, bias=C("BA"))
+        w = pairs("ERM2", "ERU2", "p3", CFG["WL"][t], 16)
+        tt(F("LOFF"), J8, w, ALU.min)
+        tt(ind(F("LK"), F("LOFF")), F("TOLD"), R("LA", 128, 256), ALU.max)
 
     ustage(0)
-    estage(0)
     for t in range(RO):
         gstage(t)
         argstage(t)
         lkx(t)
         if t == 0:
             for h in range(0, 2048, 512):
-                cast(R("LK", h, h + 512), R("LKI", h, h + 512))
+                cast(R("LK", h + 128, h + 640), R("LKI", h, h + 512))
         idx(t)
         znext(t)
         ystage(t)
         rec(t)
-        if t < RO - 1: gists(t)
+        if t < RO - 1:
+            gists(t)
+            ustage(t + 1)
+            mm((AA, F("W16"), F("ACC"), True, True))
+            estage(t + 1)
         far(t)
         names(t)
         links(t)
-        if t < RO - 1:
-            ustage(t + 1)
-            estage(t + 1)
-    dma("S", "yi", R("IX", 0, 1024))
-    dma("Y", "yl", R("LK", 0, 2048))
+    dma("S", "yi", WI)
+    dma("Y", "yl", WL)
     dma("Y", "yz", F("ZR"))
     m["run"]()

@@ -3,14 +3,14 @@ from concourse.mybir import AluOpType, ActivationFunctionType, AxisListType
 ALU = AluOpType
 ACT = ActivationFunctionType
 RO = 3
-SEG = [8 * c * (c + 1) for c in range(9)]
+SEG = [144 * c if c < 4 else 1136 - 160 * c for c in range(8)]
 PSUM = ("p0", "p1", "p2", "p3", "p4", "p5", "p6", "p7")
 SCRATCH = {b: ("psum", [128, 512], "float32") for b in PSUM}
 for _t, _names in {
     "float32": "IX:1152 LK:2176 IDF:128 W16:128 UU:128 THR:128 ACC:1 WLF:64 KE:8 DUMP:16 TW:32 ERF:128 ERF2:128 NA:256 LA:256 TOLD:128",
     "bfloat16": "XC:2048 GI:1152 Z0:128 Z1:128 Z2:128 ZR:128 ZN0:128 ZN1:128 ZN2:128 ZH:128 ZS:2048 ZREP:2048 ZT0:128 ZT1:128 RM:512 MK:1024 RX:1024 RD:576 XA:576 XS:576 J32:512 "
                 "ONESB:128 DIF:144 RQ:128 HQ:128 IDB:144 NIDB:128 P4K:128 N4K:128 HID:128 BOB:128 M16:128 TH16:128 RS:128 RC:128 CRI:128 CRL:128 UT:128 "
-                "G8:64 R1:576 R2:576 WB:128 QB:128 DG:2048 AG:2048 DY:2048 AY:2048 GR:1024 XG:2064 XM:2048 AF:2048 CMP:128 CNS:128 RS8:8 NRM:128 SG:128 STEP:144",
+                "G8:64 R2:576 WB:128 QB:128 DG:2048 AG:2048 DY:2048 AY:2048 GR:1024 XG:2064 XM:2048 AF:2048 CMP:128 CNS:128 RS8:8 NRM:128 SG:128 STEP:144 ACX:128 W16B:128",
     "float16": "PD:128 QD:128 TD:128 TB:128 DL:8 PW:128 QW:128 VH0:128 VH1:128 EH:128 ERM:128 ERU:128 ERM2:128 ERU2:128 JH0:128 JH1:128 LG:2048",
     "int32": "IXI:1024 LKI:2048 WTI:1 HKI:2 THI:2 PIO:1 PR:3 CIO:32 PWI:128 QWI:128 VI:128 EI:128 KMIN:128 KA:8 KMX:128 KJ:8",
     "uint16": "OFFG:16 ENDS:2 EU:128 E8U:8 JU:128 NU:128 GOFF:8 NOFF:8 LOFF:8 JX8:8",
@@ -19,7 +19,7 @@ for _t, _names in {
         SCRATCH[_n.split(":")[0]] = ("sbuf", [128, int(_n.split(":")[1])], _t)
 PART = {}
 _at = 0
-for _n in "RF:1 P32:1 P16:1 PF:1 WC:1 HKF:2 THF:2 NM15:1 K0:1 BA:1 BB:1 EN:1 C4K:8".split():
+for _n in "RF:1 P32:1 P16:1 PF:1 WC:1 HKF:2 THF:2 NM15:1 K0:1 BA:1 BB:1 EN:2 C4K:8".split():
     PART[_n.split(":")[0]] = _at
     _at += int(_n.split(":")[1])
 SCRATCH["CF"] = ("sbuf", [128, _at], "float32")
@@ -27,10 +27,11 @@ SEMAPHORES = ["sv", "ss", "sp", "sg", "ls", "za1", "za2", "zr"] + ["d%d" % i for
 TWO = ("bfloat16", "float16", "uint16")
 COSTS = [dict(cy=0.85, pe=0.42, ga=1.4, sc=3.0, wake=180.0, same=150.0, fx=40.0, dma=1000.0, bw=450.0, rem=2500.0),
          dict(cy=0.83, pe=0.42, ga=1.1, sc=2.0, wake=250.0, same=150.0, fx=40.0, dma=1500.0, bw=350.0, rem=3500.0),
-         dict(cy=1.1, pe=0.55, ga=1.9, sc=5.0, wake=150.0, same=120.0, fx=40.0, dma=1500.0, bw=300.0, rem=2000.0)]
-TRIALS = 5000
-CFG = dict(G=["S01 W24 S12"] * 3, GS=["01 24 12"] * 3, Y=["W01 S12 W23 S34"] * 3, YS=["01 12 23 34"] * 3, X=["S01 V34 S12 S23"] * 3, L=["02 24"] * 3,
-           M=["02 24"] * 3, ZN="VVV", EI="SSS", EL="SSV", WI="SSS", WL="SSV", TO="VVV", JH="GGG", NE=8)
+         dict(cy=1.05, pe=0.52, ga=1.7, sc=4.5, wake=180.0, same=150.0, fx=40.0, dma=1500.0, bw=300.0, rem=2000.0)]
+TRIALS, STEPS = 1000, 20000
+CFG = dict(G=["S01 W24 S12"] * 3, GS=["D24 A01 P24 A12"] * 3, Y=["W01 S12 W23 S34"] * 3, YS=["D01 P01 D23 A12 P23 A34"] * 3,
+           RF="SSV", EA="-XX", ZS="VGG", LB=[(("p0", 0), ("p0", 384))] * 2 + [(("p2", 0), ("p5", 0))], X=["S01 S12 S23 S34"] * 3, L=["01 12 23 34"] * 3,
+           M=["02 23 34"] * 3, ZN="VVV", EI="SSS", EL="SSV", WI="SSS", WL="SSS", TO="VVV", JH="GGG", NE=8)
 ORDER = {}
 
 
@@ -129,7 +130,72 @@ def schedule(ops):
         if it == 0: base = [length(order, s) for s in range(len(COSTS))]
         e = sum([length(order, s) / base[s] for s in range(len(COSTS))])
         if e < best[0]: best = (e, order, key, look)
-    return [length(best[1], s) for s in range(len(COSTS))], best[1]
+
+    def held(order, s):
+        c, la, (wk, sm) = cost[s], lat[s], hop[s]
+        fin, sta, free, why, last = [0.0] * n, [0.0] * n, {}, [None] * n, {}
+        for i in order:
+            q = que[i]
+            t = free.get(q, 0.0)
+            why[i] = (last.get(q), True)
+            for j, w in pred[i]:
+                a = (fin[j] + (sm if que[j] == q else wk)) if w else sta[j]
+                if a > t: t, why[i] = a, (j, False)
+            last[q] = i
+            sta[i] = t
+            free[q] = t + c[i]
+            fin[i] = t + c[i] + la[i]
+        i = max(range(n), key=lambda k: fin[k])
+        out = []
+        while why[i][0] is not None:
+            if why[i][1]: out.append((why[i][0], i))
+            i = why[i][0]
+        return out
+
+    def ahead(order, j, i):
+        a, b = order.index(j), order.index(i)
+        need, qs = set(k for k, w in pred[i]), set()
+        move = []
+        for k in reversed(order[a:b]):
+            if k in need or que[k] in qs:
+                if k == j: return None
+                move.append(k)
+                need.update(x for x, w in pred[k])
+                qs.add(que[k])
+        mv = set(move)
+        return order[:a] + move[::-1] + [i] + [k for k in order[a:b] if k not in mv] + order[b + 1:]
+
+    def behind(order, j, i):
+        a, b = order.index(j), order.index(i)
+        need, qs = set(k for k, w in succ[j]), set()
+        move = []
+        for k in order[a + 1:b + 1]:
+            if k in need or que[k] in qs:
+                if k == i: return None
+                move.append(k)
+                need.update(x for x, w in succ[k])
+                qs.add(que[k])
+        mv = set(move)
+        return order[:a] + [k for k in order[a + 1:b + 1] if k not in mv] + [j] + move + order[b + 1:]
+
+    now, top, cand = best[:2], best[:2], []
+    for it in range(STEPS):
+        if not cand: cand = held(now[1], int(rand() * 2.999))
+        j, i = cand[int(rand() * (len(cand) - 0.001))]
+        x = rand()
+        if x < 0.3:
+            mine = [k for k in now[1][:now[1].index(j) + 1] if que[k] == que[i]]
+            j = mine[max(0, len(mine) - 2 - int(5 * rand()))]
+        if x > 0.7:
+            mine = [k for k in now[1][now[1].index(i):] if que[k] == que[i]]
+            order = behind(now[1], j, mine[min(len(mine) - 1, int(8 * rand()))])
+        else: order = ahead(now[1], j, i)
+        if order is None: continue
+        e = sum([length(order, s) / base[s] for s in range(len(COSTS))])
+        if e < now[0] + 0.006 * (1 - it / STEPS) * rand():
+            now, cand = (e, order), []
+            if e < top[0]: top = now
+    return [length(top[1], s) for s in range(len(COSTS))], top[1]
 
 
 def make(g, T):
@@ -285,10 +351,10 @@ def rank_program(g, core, T, topo):
     END = lambda b: R(b, 15, 128, 16)
     C8, REP, LAST = G8(0), R("OFFG", 0, 8), R("OFFG", 8, 16)
     WEIGHT = {32768: G8(1), -32768: G8(2), 65536: G8(3), -65536: G8(4), 1: G8(0)}
-    PU, PU2, PE, AA = R("p0", 0, 128), R("p0", 128, 256), R("p0", 256, 384), R("p0", 128, 129)
+    PU, PU2, PE, AA = R("p0", 0, 128), R("p0", 128, 256), R("p3", 384, 512), R("p3", 128, 129)
     PT, PV = R("p6", 0, 128), R("p6", 128, 256)
     KEY, E8, GD8 = R("p1", 0, 128), R("p1", 128, 136), R("p1", 136, 144)
-    PZ, J8, PLA = R("p3", 128, 256), R("p3", 64, 72), R("p3", 384, 512)
+    PZ, J8 = R("p3", 128, 256), R("p3", 64, 72)
     FT, PNA = R("p4", 128, 256), R("p4", 256, 512)
     WI, WL, WX, WG = R("IX", 128, 1152), R("LK", 128, 2176), F("XC"), R("GI", 128, 1152)
     IDB, SHB, NIDB, P4K, N4K, ONES = R("IDB", 0, 128), R("IDB", 1, 129), F("NIDB"), F("P4K"), F("N4K"), F("ONESB")
@@ -349,17 +415,17 @@ def rank_program(g, core, T, topo):
         iota(R(b, 0, 128), [[0, 128]], 0, 0)
     iota(R("XG", 2048, 2064), [[0, 16]], 0, 0)
     iota(R("STEP", 0, 16), [[0, 16]], 1, 0)
-    iota(F("W16"), [[0, 128]], 16, 0)
+    iota(F("W16" if "C" in CFG["EA"] else "W16B"), [[0, 128]], 16, 0)
     act(F("UT"), R("DIF", 0, 128), ACT.Sign, bias=0.5)
     act(D8("C4K"), C8, ACT.Copy, scale=4096.0)
-    iota(F("RD"), [[0, 576]], 0, 0)
+    fill(F("RD"), 0.0)
+    fill(R("RD", 0, 576, 144), 1.0e6)
+    fill(R("RD", 16, 576, 160), 1.0e6)
     for c in range(8):
-        cast(R("R1", SEG[c], SEG[c + 1]), R("P4K", 0, 16 * c + 16))
-        act(R("R2", SEG[c], SEG[c + 1]), R("UT", 0, 16 * c + 16), ACT.Copy, scale=C("C4K", c))
-        iota(C("RD", SEG[c]), [[0, 1]], 1 << 20, 0)
-    act(C("EN"), C("RF"), ACT.Square, bias=1.5)
-    ts(C("EN"), C("EN"), 8.0, ALU.mult, -3.0, ALU.add)
-    ts(C("ENDS"), C("EN"), 575.0, ALU.min)
+        act(R("R2", SEG[c], SEG[c] + 16 * c + 16), R("UT", 0, 16 * c + 16), ACT.Copy, scale=C("C4K", c))
+    act(C("EN", 0), C("RF"), ACT.Copy, scale=160.0, bias=15.0)
+    act(C("EN", 1), C("RF"), ACT.Copy, scale=-144.0, bias=1151.0)
+    tt(C("ENDS"), C("EN", 0), C("EN", 1), ALU.min)
     ts(F("DUMP"), R("CIO", 16, 32), C("RF"), ALU.add)
     ts(F("DL"), C8, C("PF"), ALU.mult)
     ts(C("K0"), C("RF"), 0.0, ALU.is_equal, 4096.0, ALU.mult)
@@ -381,7 +447,10 @@ def rank_program(g, core, T, topo):
         act(F("QB"), PU, ACT.Copy, bias=191.5, scale=1 / 4096)
         mm((PU2, F("WB"), z, True, False), (PU2, N4K, F("QB"), False, True))
         act(F("UU"), PU2, ACT.Square, bias=784384.0)
-        if t: mm((PE, F("PW"), z, True, False), (PE, F("IDF"), F("UU"), False, True))
+        if CFG["EA"][t] == "C": mm((PE, F("PW"), z, True, False), (PE, F("IDF"), F("UU"), False, True))
+        elif t:
+            act(F("ACX"), ONES, ACT.Identity, scale=F("ACC"), bias=8.0)
+            mm((PE, F("PW"), z, True, False), (PE, F("ACX"), F("W16B"), False, True))
         else:
             mm((PE, F("PW"), z, True, True))
             estage(0)
@@ -393,11 +462,13 @@ def rank_program(g, core, T, topo):
         cast(F("VH%d" % (t & 1)), F("VI"))
         for w, a, b in plan("G", t):
             if w != "S":
-                cp(R("ZS", 512 * a, 512 * b, 16), R("Z%d" % t, 32 * a, 32 * b))
+                (cast if CFG["ZS"][t] == "G" else cp)(R("ZS", 512 * a, 512 * b, 16), R("Z%d" % t, 32 * a, 32 * b))
                 scan(R("ZREP", 512 * a, 512 * b), R("RX", 0, 512 * (b - a)), R("ZS", 512 * a, 512 * b), ALU.mult, ALU.add)
 
     def estage(t):
-        if t: ts(F("EI"), PE, AA, ALU.add, 16384.0, ALU.add)
+        if CFG["EA"][t] == "C":
+            mm((AA, F("W16"), F("ACC"), True, True))
+            ts(F("EI"), PE, AA, ALU.add, 16384.0, ALU.add)
         else: tt(F("EI"), PE, F("UU"), ALU.add)
         ts(F("EI"), F("EI"), 5, ALU.arith_shift_right, 1023, ALU.bitwise_and)
         cp(F("EU"), F("EI"))
@@ -423,13 +494,12 @@ def rank_program(g, core, T, topo):
                 if who == "V": act(R(AG, a, b), R(DG, a, b), ACT.Abs)
                 else: ts(R(AG, a, b), R(DG, a, b), 0.0, ALU.max)
 
-    def lanesum(out, x, a, b, pos, ks, w):
-        for (buf, wt) in ((("D" + x, -w), ("A" + x, 2 * w)) if pos else (("A" + x, w),)):
-            mm(*[(R(out[0], out[1] + k, out[1] + 128, 16, 32 * a, 32 * b), R(buf, 512 * a + k, 512 * b, 16), WEIGHT[wt], False, False) for k in range(ks)])
+    def lanesum(out, buf, a, b, ks, w):
+        mm(*[(R(out[0], out[1] + k, out[1] + 128, 16, 32 * a, 32 * b), R(buf, 512 * a + k, 512 * b, 16), WEIGHT[w], False, False) for k in range(ks)])
 
     def sums(out, x, t, ks, w):
-        for (_, a, b) in plan(x + "S", t):
-            lanesum(out, x, a, b, any(who == "W" and q <= a < e for who, q, e in plan(x, t)), ks, w)
+        for (what, a, b) in plan(x + "S", t):
+            lanesum(out, ("D" if what == "D" else "A") + x, a, b, ks, {"A": w, "P": 2 * w, "D": -w}[what])
 
     def gstage(t):
         mm((KEY, ONES, F("CRI"), True, False))
@@ -460,15 +530,17 @@ def rank_program(g, core, T, topo):
             else: cp(o, lst)
 
     def pairs(masked, plain, bank, who, x):
-        for (a, b, P) in ((0, 448, R("p6", 0, 448)), (448, 576, R(bank, 256, 384))):
-            mm((P, F(plain), R("R1", a, b), True, False), (P, F(masked), R("R2", a, b), False, True))
+        seg = lambda c: R("p6", SEG[c], SEG[c] + 16 * c + 16) if SEG[c] < 432 else R(bank, SEG[c] - 224, SEG[c] - 208 + 16 * c)
+        for (a, b, P) in ((0, 432, R("p6", 0, 432)), (432, 576, R(bank, 208, 352))):
+            cs = [c for c in range(8) if a <= SEG[c] < b]
+            mm((P, F(masked), R("R2", a, b), True, False), *[(seg(c), F(plain), R("P4K", 0, 16 * c + 16), False, c == cs[-1]) for c in cs])
             if who == "S": act(R("XA", a, b), P, ACT.Abs)
         if who == "S":
             scan(F("XS"), F("RD"), F("XA"), ALU.max, ALU.min)
             tt(R("TW", x, x + 16), ind(F("XS"), C("ENDS")), F("DUMP"), ALU.add)
         else:
             for c in range(8):
-                least(C("TW", x + 8 + c), R("p6", SEG[c], SEG[c + 1]) if c < 7 else R(bank, 256, 384))
+                least(C("TW", x + 8 + c), seg(c))
             tt(R("TW", x, x + 8), R("TW", x + 8, x + 16), D8("DUMP"), ALU.add)
         return R("TW", x, x + 8)
 
@@ -479,10 +551,7 @@ def rank_program(g, core, T, topo):
             act(F("ERF"), ind(S8(7), REP), ACT.Copy)
             cast(F("ERU"), F("ERF"))
         w = pairs("ERM", "ERU", "p1", CFG["WI"][t], 0)
-        if t < RO - 1:
-            tt(S8(1), E8, w, ALU.min)
-            cp(F("NOFF"), S8(1))
-        else: tt(F("NOFF"), E8, w, ALU.min)
+        tt(F("NOFF"), E8, w, ALU.min)
 
     def znext(t):
         for (_, a, b) in plan("M", t):
@@ -519,12 +588,12 @@ def rank_program(g, core, T, topo):
 
     def gists(t):
         mm((GD8, IDB, G8(7), True, False), (GD8, F("NRM"), F("DL"), False, True))
-        tt(F("GOFF"), GD8, S8(1), ALU.min)
+        tt(F("GOFF"), GD8, F("NOFF"), ALU.min)
         cp(ind(F("GI"), F("GOFF")), F("Z%d" % t))
 
     def names(t):
         mm((FT, ONES, F("TB"), True, False))
-        lanesum(FT, "F", 0, 4, False, 16, 1)
+        lanesum(FT, "AF", 0, 4, 16, 1)
         mm(*[(R("p4", 128 + k, 256, 16), P4K, F("RS8"), False, k == 15) for k in range(16)])
         act(F("SG"), FT, ACT.Sign, bias=4095.5)
         a, b = R("p4", 256, 384), R("p4", 384, 512)
@@ -534,7 +603,9 @@ def rank_program(g, core, T, topo):
 
     def links(t):
         ts(F("KJ"), END("KMX"), 2047, ALU.bitwise_and)
-        act(S8(2), F("RS8"), ACT.Copy, scale=-2048.5, bias=-2047.5)
+        if CFG["RF"][t] == "S": act(S8(2), F("RS8"), ACT.Copy, scale=-2048.5, bias=-2047.5)
+        else: ts(S8(2), END("CNS"), -8192.0, ALU.mult, 1.0, ALU.min)
+        PLA, PLB = [R(b, x, x + 128) for b, x in CFG["LB"][t]]
         tt(S8(3), F("KJ"), S8(2), ALU.add)
         tt(F("ERM2"), ind(S8(3), REP), F("NRM"), ALU.mult)
         if CFG["EL"][t] == "V": ts(F("ERU2"), ind(S8(3), REP), 0.0, ALU.max)
@@ -546,8 +617,10 @@ def rank_program(g, core, T, topo):
         now, was = R("STEP", 16, 144), R("STEP", 15, 143)
         mm((J8, IDB, G8(6), True, False), (J8, F("ERM2"), C8, False, True))
         ts(F("JX8"), J8, -128.0, ALU.add)
-        mm((PZ, SHB, F("JH%d" % (t & 1)), True, False), (PZ, now, P4K, False, False), (PZ, was, N4K, False, True))
-        act(R("LA", 128, 256), PZ, ACT.Identity, bias=C("BB"))
+        w = pairs("ERM2", "ERU2", "p3", CFG["WL"][t], 16)
+        tt(F("LOFF"), J8, w, ALU.min)
+        mm((PLB, SHB, F("JH%d" % (t & 1)), True, False), (PLB, now, P4K, False, False), (PLB, was, N4K, False, True))
+        act(R("LA", 128, 256), PLB, ACT.Identity, bias=C("BB"))
         if CFG["TO"][t] == "V":
             mm((PLA, now, N4K, True, False), (PLA, was, P4K, False, True))
             act(R("LA", 0, 128), PLA, ACT.Identity, bias=C("BA"))
@@ -556,8 +629,6 @@ def rank_program(g, core, T, topo):
             act(R("LA", 0, 128), ind(WL, F("JX8")), ACT.Copy)
             mm((PLA, now, N4K, True, False), (PLA, was, P4K, False, False), (PLA, F("IDF"), R("LA", 0, 128), False, True))
             act(F("TOLD"), PLA, ACT.Identity, bias=C("BA"))
-        w = pairs("ERM2", "ERU2", "p3", CFG["WL"][t], 16)
-        tt(F("LOFF"), J8, w, ALU.min)
         tt(ind(F("LK"), F("LOFF")), F("TOLD"), R("LA", 128, 256), ALU.max)
 
     ustage(0)
@@ -575,7 +646,6 @@ def rank_program(g, core, T, topo):
         if t < RO - 1:
             gists(t)
             ustage(t + 1)
-            mm((AA, F("W16"), F("ACC"), True, True))
             estage(t + 1)
         far(t)
         names(t)

from concourse.mybir import AluOpType, ActivationFunctionType, AxisListType

ALU = AluOpType
ACT = ActivationFunctionType
RO = 3
SEG = [144 * c if c < 4 else 1136 - 160 * c for c in range(8)]
PSUM = ("p0", "p1", "p2", "p3", "p4", "p5", "p6", "p7")
SCRATCH = {b: ("psum", [128, 512], "float32") for b in PSUM}
for _t, _names in {
    "float32": "IX:1152 LK:2176 IDF:128 W16:128 UU:128 THR:128 ACC:1 WLF:64 KE:8 DUMP:16 TW:32 ERF:128 ERF2:128 NA:256 LA:256 TOLD:128",
    "bfloat16": "XC:2048 GI:1152 Z0:128 Z1:128 Z2:128 ZR:128 ZN0:128 ZN1:128 ZN2:128 ZH:128 ZS:2048 ZREP:2048 ZT0:128 ZT1:128 RM:512 MK:1024 RX:1024 RD:576 XA:576 XS:576 J32:512 "
                "ONESB:128 DIF:144 RQ:128 HQ:128 IDB:144 NIDB:128 P4K:128 N4K:128 HID:128 BOB:128 M16:128 TH16:128 RS:128 RC:128 CRI:128 CRL:128 UT:128 "
                "G8:64 R2:576 WB:128 QB:128 DG:2048 AG:2048 DY:2048 AY:2048 GR:1024 XG:2064 XM:2048 AF:2048 CMP:128 CNS:128 RS8:8 NRM:128 SG:128 STEP:144 ACX:128 W16B:128",
    "float16": "PD:128 QD:128 TD:128 TB:128 DL:8 PW:128 QW:128 VH0:128 VH1:128 EH:128 ERM:128 ERU:128 ERM2:128 ERU2:128 JH0:128 JH1:128 LG:2048",
    "int32": "IXI:1024 LKI:2048 WTI:1 HKI:2 THI:2 PIO:1 PR:3 CIO:32 PWI:128 QWI:128 VI:128 EI:128 KMIN:128 KA:8 KMX:128 KJ:8",
    "uint16": "OFFG:16 ENDS:2 EU:128 E8U:8 JU:128 NU:128 GOFF:8 NOFF:8 LOFF:8 JX8:8",
}.items():
    for _n in _names.split():
        SCRATCH[_n.split(":")[0]] = ("sbuf", [128, int(_n.split(":")[1])], _t)
PART = {}
_at = 0
for _n in "RF:1 P32:1 P16:1 PF:1 WC:1 HKF:2 THF:2 NM15:1 K0:1 BA:1 BB:1 EN:2 C4K:8".split():
    PART[_n.split(":")[0]] = _at
    _at += int(_n.split(":")[1])
SCRATCH["CF"] = ("sbuf", [128, _at], "float32")
SEMAPHORES = ["sv", "ss", "sp", "sg", "ls", "za1", "za2", "zr"] + ["d%d" % i for i in range(16)]
TWO = ("bfloat16", "float16", "uint16")
COSTS = [dict(cy=0.85, pe=0.42, ga=1.4, sc=3.0, wake=180.0, same=150.0, fx=40.0, dma=1000.0, bw=450.0, rem=2500.0),
         dict(cy=0.83, pe=0.42, ga=1.1, sc=2.0, wake=250.0, same=150.0, fx=40.0, dma=1500.0, bw=350.0, rem=3500.0),
         dict(cy=1.05, pe=0.52, ga=1.7, sc=4.5, wake=180.0, same=150.0, fx=40.0, dma=1500.0, bw=300.0, rem=2000.0)]
TRIALS, STEPS = 1000, 20000
CFG = dict(G=["S01 W24 S12"] * 3, GS=["D24 A01 P24 A12"] * 3, Y=["W01 S12 W23 S34"] * 3, YS=["D01 P01 D23 A12 P23 A34"] * 3,
           RF="SSV", EA="-XX", ZS="VGG", LB=[(("p0", 0), ("p0", 384))] * 2 + [(("p2", 0), ("p5", 0))], X=["S01 S12 S23 S34"] * 3, L=["01 12 23 34"] * 3,
           M=["02 23 34"] * 3, ZN="VVV", EI="SSS", EL="SSV", WI="SSS", WL="SSS", TO="VVV", JH="GGG", NE=8)
ORDER = {}


def R(buf, c0, c1, step=1, p0=0, p1=128):
    if buf in PART:
        return ("CF", PART[buf] + c0, PART[buf] + c1, step, p0, p1)
    return (buf, c0, c1, step, p0, p1)


def ind(win, off): return ("ind", win, off)
def wid(r): return 16 * (r[2][2] - r[2][1]) if len(r) == 3 else (r[2] - r[1] + r[3] - 1) // r[3]
def kind(r): return SCRATCH[(r[1] if len(r) == 3 else r)[0]][2]


def schedule(ops):
    n = len(ops)
    rnd = [12345]

    def rand():
        rnd[0] = (rnd[0] * 1103515245 + 12345) & 0x7fffffff
        return (rnd[0] >> 8) / 0x7fffff

    que = [o["q"] for o in ops]
    succ = [[] for _ in range(n)]
    pred = [list(o["pre"].items()) for o in ops]
    for i in range(n):
        for j, w in pred[i]: succ[j].append((i, w))
    cost, lat, hop = [], [], []
    for C in COSTS:
        cost.append([o["f"][0] + C["cy"] * (o["f"][1] + C["ga"] * o["f"][2] + C["sc"] * o["f"][3]) + C["pe"] * o["f"][4] + o["lat"][1] / C["bw"] + C["fx"] * (o["q"] in "VS") for o in ops])
        lat.append([o["lat"][0] * C["dma"] + o["lat"][2] * C["rem"] for o in ops])
        hop.append((C["wake"], C["same"]))

    def length(order, s):
        c, la, (wk, sm) = cost[s], lat[s], hop[s]
        fin, sta, free, end = [0.0] * n, [0.0] * n, {}, 0.0
        for i in order:
            q = que[i]
            t = free.get(q, 0.0)
            for j, w in pred[i]:
                a = (fin[j] + (sm if que[j] == q else wk)) if w else sta[j]
                if a > t: t = a
            sta[i] = t
            free[q] = t + c[i]
            fin[i] = t + c[i] + la[i]
            if fin[i] > end: end = fin[i]
        return end

    pri = [0.0] * n
    for i in range(n - 1, -1, -1):
        pri[i] = cost[0][i] + lat[0][i]
        for k, w in succ[i]:
            d = cost[0][i] + (lat[0][i] + hop[0][que[k] == que[i]] if w else 0)
            if d + pri[k] > pri[i]: pri[i] = d + pri[k]

    def greedy(key, look):
        c, la, (wk, sm) = cost[0], lat[0], hop[0]
        left = [len(p) for p in pred]
        ready, rt, free, order = {}, [0.0] * n, {}, []
        for i in range(n):
            if not left[i]: ready.setdefault(que[i], []).append(i)
        while len(order) < n:
            bq, bt = None, 1e18
            for q, L in ready.items():
                if L:
                    t = max(free.get(q, 0.0), min([rt[i] for i in L]))
                    if t < bt: bq, bt = q, t
            L = ready[bq]
            best = max([i for i in L if rt[i] <= bt + look], key=lambda i: key[i])
            L.remove(best)
            s = max(bt, rt[best])
            e = s + c[best]
            free[bq] = e
            order.append(best)
            e += la[best]
            for k, w in succ[best]:
                a = (e + (sm if que[k] == bq else wk)) if w else s
                if a > rt[k]: rt[k] = a
                left[k] -= 1
                if not left[k]: ready.setdefault(que[k], []).append(k)
        return order

    best = (1e18, None, None, 0.0)
    for it in range(TRIALS):
        if it <= TRIALS // 5:
            amp = 0.0 if it == 0 else 2000.0 * rand()
            key = [p + amp * (rand() - 0.5) for p in pri]
            look = 0.0 if it == 0 else 400.0 * rand()
        else:
            key, look = list(best[2]), best[3]
            share = 0.01 if rand() < 0.5 else 0.06
            for i in range(n):
                if rand() < share: key[i] += 4000.0 * (rand() - 0.5)
            if rand() < 0.2: look = 400.0 * rand()
        order = greedy(key, look)
        if it == 0: base = [length(order, s) for s in range(len(COSTS))]
        e = sum([length(order, s) / base[s] for s in range(len(COSTS))])
        if e < best[0]: best = (e, order, key, look)

    def held(order, s):
        c, la, (wk, sm) = cost[s], lat[s], hop[s]
        fin, sta, free, why, last = [0.0] * n, [0.0] * n, {}, [None] * n, {}
        for i in order:
            q = que[i]
            t = free.get(q, 0.0)
            why[i] = (last.get(q), True)
            for j, w in pred[i]:
                a = (fin[j] + (sm if que[j] == q else wk)) if w else sta[j]
                if a > t: t, why[i] = a, (j, False)
            last[q] = i
            sta[i] = t
            free[q] = t + c[i]
            fin[i] = t + c[i] + la[i]
        i = max(range(n), key=lambda k: fin[k])
        out = []
        while why[i][0] is not None:
            if why[i][1]: out.append((why[i][0], i))
            i = why[i][0]
        return out

    def ahead(order, j, i):
        a, b = order.index(j), order.index(i)
        need, qs = set(k for k, w in pred[i]), set()
        move = []
        for k in reversed(order[a:b]):
            if k in need or que[k] in qs:
                if k == j: return None
                move.append(k)
                need.update(x for x, w in pred[k])
                qs.add(que[k])
        mv = set(move)
        return order[:a] + move[::-1] + [i] + [k for k in order[a:b] if k not in mv] + order[b + 1:]

    def behind(order, j, i):
        a, b = order.index(j), order.index(i)
        need, qs = set(k for k, w in succ[j]), set()
        move = []
        for k in order[a + 1:b + 1]:
            if k in need or que[k] in qs:
                if k == i: return None
                move.append(k)
                need.update(x for x, w in succ[k])
                qs.add(que[k])
        mv = set(move)
        return order[:a] + [k for k in order[a + 1:b + 1] if k not in mv] + [j] + move + order[b + 1:]

    now, top, cand = best[:2], best[:2], []
    for it in range(STEPS):
        if not cand: cand = held(now[1], int(rand() * 2.999))
        j, i = cand[int(rand() * (len(cand) - 0.001))]
        x = rand()
        if x < 0.3:
            mine = [k for k in now[1][:now[1].index(j) + 1] if que[k] == que[i]]
            j = mine[max(0, len(mine) - 2 - int(5 * rand()))]
        if x > 0.7:
            mine = [k for k in now[1][now[1].index(i):] if que[k] == que[i]]
            order = behind(now[1], j, mine[min(len(mine) - 1, int(8 * rand()))])
        else: order = ahead(now[1], j, i)
        if order is None: continue
        e = sum([length(order, s) / base[s] for s in range(len(COSTS))])
        if e < now[0] + 0.006 * (1 - it / STEPS) * rand():
            now, cand = (e, order), []
            if e < top[0]: top = now
    return [length(top[1], s) for s in range(len(COSTS))], top[1]


def make(g, T):
    eng = {"V": g.vector, "S": g.scalar, "P": g.tensor, "G": g, "Y": g.sync}
    own = {"V": "sv", "S": "ss", "P": "sp", "G": "sg"}
    ops, hist = [], {}

    def ap(r):
        if len(r) == 3:
            return ap(r[1]).indirect(ap(r[2]))
        b, c0, c1, s, p0, p1 = r
        return T[b][p0:p1, c0:c1] if s == 1 else T[b][p0:p1, c0:c1:s]

    def add(q, outs, ins, call, f, lat=(0, 0, 0), sem=None, inc=1, extra=()):
        i = len(ops)
        acc = []
        for r in ins:
            if isinstance(r, tuple):
                acc += [(r[1], False), (r[2], False)] if len(r) == 3 else [(r, False)]
        for r in outs:
            acc += [(r[1], True), (r[2], False)] if len(r) == 3 else [(r, True)]
        pre = dict(extra)
        for r, w in acc:
            ps = r[0] in PSUM
            h = hist.setdefault(r[0], [])
            for (j, r2, w2) in h:
                if j == i: continue
                q2 = ops[j]["q"]
                if ps:
                    if q == q2 == "P": wait = False
                    elif q == q2 and not (w or w2): continue
                    else: wait = not (q == q2 and not w2)
                else:
                    if not (w or w2) or r[1] >= r2[2] or r2[1] >= r[2] or r[4] >= r2[5] or r2[4] >= r[5]: continue
                    if r[3] == r2[3] and r[3] > 1 and (r[1] - r2[1]) % r[3]: continue
                    wait = not (q == q2 and not w2)
                pre[j] = pre.get(j, False) or wait
            if ps and q == "P": h[:] = []
            elif w and not ps and r[3] == 1:
                h[:] = [a for a in h if a[0] == i or not (a[1][1] >= r[1] and a[1][2] <= r[2] and a[1][4] >= r[4] and a[1][5] <= r[5])]
            h.append((i, r, w))
        name = (outs[0][1][0] + "!" if len(outs[0]) == 3 else outs[0][0]) if outs else "-"
        ops.append(dict(q=q, call=call, f=tuple(f) + (0,) * (5 - len(f)), lat=lat, pre=pre, sem=sem or own.get(q), inc=inc, name=name))
        return i

    def sc(x): return ap(x) if isinstance(x, tuple) else x

    def vcost(out, in_, f):
        n = wid(out)
        if len(out) == 3: return (50, 0, 0, n)
        if len(in_) == 3: return (50, 0, n)
        return (0, max(64, n * f))

    def half(*rs): return 0.5 if all(kind(r) in TWO for r in rs) else 1.0

    def cp(out, in_): add("V", [out], [in_], lambda n: n.tensor_copy(ap(out), ap(in_)), vcost(out, in_, half(out, in_)))

    def tt(out, a, b, o):
        add("V", [out], [a, b], lambda n: n.tensor_tensor(ap(out), ap(a), ap(b), o), vcost(out, a, 1.0 if a[0] in PSUM or b[0] in PSUM else 2.0))

    def ts(out, a, s1, o1, s2=None, o2=None):
        c = vcost(out, a, half(out, a))
        if o2 is None: add("V", [out], [a, s1], lambda n: n.tensor_scalar(ap(out), ap(a), sc(s1), None, o1), c)
        else: add("V", [out], [a, s1, s2], lambda n: n.tensor_scalar(ap(out), ap(a), sc(s1), sc(s2), o1, o2), c)

    def scan(out, a, b, o1, o2):
        add("V", [out], [a, b], lambda n: n.tensor_tensor_scan(ap(out), ap(a), ap(b), 0.0, o1, o2), vcost(out, a, half(out, a, b)))

    def least(out, in_):
        add("V", [out], [in_], lambda n: n.tensor_reduce(ap(out), ap(in_), AxisListType.X, ALU.min, apply_absolute_value=True), (0, max(64, wid(in_))))

    def fill(out, v): add("V", [out], [], lambda n: n.memset(ap(out), v), vcost(out, out, half(out)))

    def act(out, in_, f, bias=0.0, scale=1.0, acc=None):
        c = (65, 0, wid(out)) if len(in_) == 3 else (0 if acc is None else 20, max(64, wid(out)))
        if acc is None: add("S", [out], [in_, bias, scale], lambda n: n.activation(ap(out), ap(in_), f, bias=sc(bias), scale=sc(scale)), c)
        else: add("S", [out, acc], [in_, bias, scale], lambda n: n.activation(ap(out), ap(in_), f, bias=sc(bias), scale=sc(scale), accum_out=ap(acc)), c)

    def mm(*group):
        def call(n):
            for (o, l, r, a, b) in group:
                x = n.matmul(ap(o), ap(l), ap(r), a, b)
            return x
        c = sum(max(min(64, wid(l)), wid(r)) * (4 if kind(l) == "float32" else 1) for (o, l, r, a, b) in group)
        add("P", [x[0] for x in group], [x[1] for x in group] + [x[2] for x in group], call, (0, 0, 0, 0, c))

    def iota(out, pat, base, cm): add("G", [out], [], lambda n: n.iota(ap(out), pat, base, cm, allow_small_or_imprecise_dtypes=True), (130, 2 * wid(out)))
    def asel(out, in_, pat, o, fillv, base, cm): add("G", [out], [in_], lambda n: n.affine_select(ap(out), ap(in_), pat, o, fillv, base, cm), (170, 2 * wid(out)))

    def cast(out, in_): asel(out, in_, [[0, wid(out)]], ALU.is_gt, 0.0, 1, 0)

    nd = [0, None]

    def dma(q, out, in_):
        sem = "d%d" % nd[0]
        nd[0] += 1
        load = isinstance(in_, str)
        o = ap(out) if load else T[out][:]
        x = T[in_][:] if load else ap(in_)
        s = out if load else in_
        by = wid(s) * 128 * (2 if kind(s) in TWO else 4)
        i = add(q, [], [] if load else [in_], lambda n: n.dma_start(o, x), (60,), (0, 0, 0), sem, 16)
        nd[1] = add("dq", [out] if load else [], [], None, (0,), (1, by, 0), sem, 0, [(i, True)] + ([(nd[1], False)] if load and nd[1] is not None else []))

    def send(out, in_, rsem, dst, src, topo):
        rid, pid, _ = topo.addr(dst)
        en = topo.engines(src, dst)[:CFG["NE"]]
        i = add("G", [], [in_], lambda n: n.remote_dma(ap(out), ap(in_), T.sem[rsem], T.sem["ls"], pid, rid, sum(1 << x for x in en)), (1000,), (0, 0, 1), "ls", len(en))
        add("net", [out], [], None, (0,), (0, 0, 0), rsem, len(en), [(i, True)])

    def run():
        if "best" not in ORDER:
            ORDER["ops"] = ops
            ORDER["best"] = schedule(ops)
        cnt, known, tok = {}, {q: {} for q in eng}, {}
        for i in ORDER["best"][1]:
            o = ops[i]
            q = o["q"]
            cnt[o["sem"]] = cnt.get(o["sem"], 0) + o["inc"]
            if q not in eng:
                tok[i] = (o["sem"], cnt[o["sem"]], {})
                continue
            k = known[q]
            waits = sorted((tok[j] for j, w in o["pre"].items() if w), key=lambda t: (t[0], -t[1]))
            waits.sort(key=lambda t: t[0] == o["sem"])
            for (s, v, snap) in waits:
                if k.get(s, 0) < v:
                    eng[q].wait_ge(T.sem[s], v)
                    k[s] = v
                    for a, b in snap.items():
                        if k.get(a, 0) < b: k[a] = b
            c = o["call"](eng[q])
            if o["sem"] != "ls": c.then_inc(T.sem[o["sem"]], o["inc"])
            tok[i] = (o["sem"], cnt[o["sem"]], dict(k))
        for s in sorted(cnt):
            if known["G"].get(s, 0) < cnt[s]: g.wait_ge(T.sem[s], cnt[s])

    return dict(cp=cp, tt=tt, ts=ts, scan=scan, least=least, fill=fill, act=act, mm=mm, iota=iota, asel=asel, cast=cast, dma=dma, send=send, run=run)


def rank_program(g, core, T, topo):
    rank = T.rank_of(core)
    if rank is None:
        return
    n = len(T.cores)
    m = make(g, T)
    cp, tt, ts, scan, least, fill, act, mm, iota, asel, cast, dma = (m[k] for k in ("cp", "tt", "ts", "scan", "least", "fill", "act", "mm", "iota", "asel", "cast", "dma"))
    F = lambda b: R(b, 0, SCRATCH[b][1][1])
    C = lambda b, i=0: R(b, i, i + 1)
    S8 = lambda i: R("WLF", 8 * i, 8 * i + 8)
    D8 = lambda b: R(b, 0, 8)
    G8 = lambda i: R("G8", 8 * i, 8 * i + 8)
    END = lambda b: R(b, 15, 128, 16)
    C8, REP, LAST = G8(0), R("OFFG", 0, 8), R("OFFG", 8, 16)
    WEIGHT = {32768: G8(1), -32768: G8(2), 65536: G8(3), -65536: G8(4), 1: G8(0)}
    PU, PU2, PE, AA = R("p0", 0, 128), R("p0", 128, 256), R("p3", 384, 512), R("p3", 128, 129)
    PT, PV = R("p6", 0, 128), R("p6", 128, 256)
    KEY, E8, GD8 = R("p1", 0, 128), R("p1", 128, 136), R("p1", 136, 144)
    PZ, J8 = R("p3", 128, 256), R("p3", 64, 72)
    FT, PNA = R("p4", 128, 256), R("p4", 256, 512)
    WI, WL, WX, WG = R("IX", 128, 1152), R("LK", 128, 2176), F("XC"), R("GI", 128, 1152)
    IDB, SHB, NIDB, P4K, N4K, ONES = R("IDB", 0, 128), R("IDB", 1, 129), F("NIDB"), F("P4K"), F("N4K"), F("ONESB")
    plan = lambda k, t: [(p[:-2], int(p[-2]), int(p[-1])) for p in CFG[k][t].split()]

    dma("Y", F("WTI"), "wt"); dma("Y", F("Z0"), "zc"); dma("Y", F("HKI"), "hk")
    dma("S", WG, "gi"); dma("Y", F("IXI"), "ix"); dma("Y", F("THI"), "th"); dma("S", F("XC"), "xc"); dma("Y", F("LKI"), "lk")

    iota(F("PIO"), [[0, 1]], 0, 1)
    iota(F("HQ"), [[16, 8], [0, 16]], 0, 0)
    iota(F("DIF"), [[1, 144]], 0, -1)
    iota(F("RQ"), [[0, 8], [1, 16]], 0, 0)
    iota(F("J32"), [[1, 32], [0, 16]], 0, 0)
    iota(R("CIO", 0, 8), [[1, 8]], 0, 0)
    iota(R("CIO", 8, 16), [[16, 8]], 15, 0)
    iota(R("CIO", 16, 32), [[16, 16]], 0, 0)
    iota(C("PF"), [[0, 1]], -2048, 1)
    for i, v in enumerate((15, 31, 112)):
        ts(C("PR", i), F("PIO"), v, ALU.bitwise_and)
    cp(R("RF", 0, 3), F("PR"))
    ts(F("BOB"), F("HQ"), C("P16"), ALU.is_equal)
    ts(F("IDB"), F("DIF"), 0.0, ALU.is_equal)
    for b, v in (("N4K", -4096), ("IDF", 1), ("NIDB", -1), ("P4K", 4096), ("HID", 255 / 512)):
        act(F(b), IDB, ACT.Copy, scale=float(v))
    fill(ONES, 1.0)
    cp(C("WC"), C("WTI"))
    ts(F("WB"), F("BOB"), C("WC"), ALU.mult)
    ts(C("HKF", 0), C("HKI", 0), 2.0, ALU.mult, -1792.0, ALU.add)
    ts(C("HKF", 1), C("HKI", 1), -1792.0, ALU.add)
    for d, w, wi, i, P in (("PD", "PW", "PWI", 0, R("p1", 128, 256)), ("QD", "QW", "QWI", 1, R("p3", 128, 256))):
        ts(F(d), IDB, C("HKF", i), ALU.mult)
        mm((P, F("BOB"), F(d), True, True))
        ts(F(wi), P, C("WC"), ALU.mult)
        ts(F(wi), F(wi), 2047, ALU.bitwise_and)
        ts(F(w), F(wi), 16.0, ALU.mult)
    ts(F("RM"), F("J32"), C("P32"), ALU.is_equal)
    ts(F("M16"), F("RQ"), C("RF"), ALU.is_equal)
    act(R("MK", 0, 128), F("M16"), ACT.Copy)
    for a in (128, 256, 512):
        act(R("MK", a, 2 * a), R("MK", 0, a), ACT.Copy)
    fill(F("RX"), 1.0)
    fill(R("RX", 0, 1024, 16), 0.0)
    act(F("RS"), R("RX", 0, 128), ACT.Copy, scale=-67108864.0, bias=33554432.0)
    act(F("RC"), R("RX", 0, 128), ACT.Copy, scale=73.5, bias=-9.5)
    act(F("TH16"), F("M16"), ACT.Copy, scale=99.0, bias=-99.0)
    act(R("CRI", 0, 128, 1, 0, 64), R("RQ", 0, 128, 1, 0, 64), ACT.Copy, scale=32.0, bias=16.0)
    fill(R("CRI", 0, 128, 1, 64, 128), -262144.0)
    act(R("CRL", 0, 128, 1, 0, 64), R("RQ", 0, 128, 1, 0, 64), ACT.Copy, scale=32.0, bias=-512.0)
    fill(R("CRL", 0, 128, 1, 64, 128), 262144.0)
    for v, r in WEIGHT.items():
        act(r, R("BOB", 0, 128, 16), ACT.Copy, scale=float(v))
    for i, v in ((5, -896), (6, 127), (7, 2048)):
        iota(G8(i), [[0, 8]], v, 0)
    cp(F("OFFG"), R("CIO", 0, 16))
    for a, b in sorted(set((a, b) for t in range(RO) for w, a, b in plan("G", t) if w != "S")):
        fill(R("ZS", 512 * a, 512 * b), 0.0)
    for b in ("IX", "LK", "GI"):
        iota(R(b, 0, 128), [[0, 128]], 0, 0)
    iota(R("XG", 2048, 2064), [[0, 16]], 0, 0)
    iota(R("STEP", 0, 16), [[0, 16]], 1, 0)
    iota(F("W16" if "C" in CFG["EA"] else "W16B"), [[0, 128]], 16, 0)
    act(F("UT"), R("DIF", 0, 128), ACT.Sign, bias=0.5)
    act(D8("C4K"), C8, ACT.Copy, scale=4096.0)
    fill(F("RD"), 0.0)
    fill(R("RD", 0, 576, 144), 1.0e6)
    fill(R("RD", 16, 576, 160), 1.0e6)
    for c in range(8):
        act(R("R2", SEG[c], SEG[c] + 16 * c + 16), R("UT", 0, 16 * c + 16), ACT.Copy, scale=C("C4K", c))
    act(C("EN", 0), C("RF"), ACT.Copy, scale=160.0, bias=15.0)
    act(C("EN", 1), C("RF"), ACT.Copy, scale=-144.0, bias=1151.0)
    tt(C("ENDS"), C("EN", 0), C("EN", 1), ALU.min)
    ts(F("DUMP"), R("CIO", 16, 32), C("RF"), ALU.add)
    ts(F("DL"), C8, C("PF"), ALU.mult)
    ts(C("K0"), C("RF"), 0.0, ALU.is_equal, 4096.0, ALU.mult)
    act(C("BA"), C("K0"), ACT.Copy, scale=-1.0)
    act(C("BB"), C("K0"), ACT.Copy, bias=-4096.0)
    ts(C("NM15"), C("RF"), 15.0, ALU.is_equal, 2000.0, ALU.mult)
    tt(C("THF", 0), C("THI", 0), C("NM15"), ALU.subtract)
    ts(C("THF", 1), C("THI", 1), -1.0, ALU.mult)
    ts(F("TD"), IDB, C("THF", 0), ALU.mult)
    ts(F("TB"), IDB, C("THF", 1), ALU.mult)
    mm((FT, ONES, F("TD"), True, True))
    act(F("THR"), FT, ACT.Copy, bias=16744448.0, scale=-32768.0)
    for h in (0, 512):
        cast(R("IX", h + 128, h + 640), R("IXI", h, h + 512))

    def ustage(t):
        z = F("Z%d" % t)
        mm((PU, F("WB"), z, True, True))
        act(F("QB"), PU, ACT.Copy, bias=191.5, scale=1 / 4096)
        mm((PU2, F("WB"), z, True, False), (PU2, N4K, F("QB"), False, True))
        act(F("UU"), PU2, ACT.Square, bias=784384.0)
        if CFG["EA"][t] == "C": mm((PE, F("PW"), z, True, False), (PE, F("IDF"), F("UU"), False, True))
        elif t:
            act(F("ACX"), ONES, ACT.Identity, scale=F("ACC"), bias=8.0)
            mm((PE, F("PW"), z, True, False), (PE, F("ACX"), F("W16B"), False, True))
        else:
            mm((PE, F("PW"), z, True, True))
            estage(0)
        mm((PT, z, NIDB, True, True))
        act(F("ZT%d" % (t & 1)), PT, ACT.Copy)
        mm((PV, F("QW"), z, True, True))
        tt(F("VI"), PV, F("UU"), ALU.add)
        ts(F("VI"), F("VI"), 4, ALU.arith_shift_right, 2047, ALU.bitwise_and)
        cast(F("VH%d" % (t & 1)), F("VI"))
        for w, a, b in plan("G", t):
            if w != "S":
                (cast if CFG["ZS"][t] == "G" else cp)(R("ZS", 512 * a, 512 * b, 16), R("Z%d" % t, 32 * a, 32 * b))
                scan(R("ZREP", 512 * a, 512 * b), R("RX", 0, 512 * (b - a)), R("ZS", 512 * a, 512 * b), ALU.mult, ALU.add)

    def estage(t):
        if CFG["EA"][t] == "C":
            mm((AA, F("W16"), F("ACC"), True, True))
            ts(F("EI"), PE, AA, ALU.add, 16384.0, ALU.add)
        else: tt(F("EI"), PE, F("UU"), ALU.add)
        ts(F("EI"), F("EI"), 5, ALU.arith_shift_right, 1023, ALU.bitwise_and)
        cp(F("EU"), F("EI"))
        cast(F("EH"), F("EI"))

    def zsub(p, t, q): return (p, R("ZT%d" % (t & 1), 0, 128, 1, 32 * q, 32 * q + 32), R("RM", 0, 512, 1, 32 * q, 32 * q + 32), True, False)

    def dist(win, off, sub, sh, pieces, t=None):
        DG, AG = ("DG", "AG") if sub == "ZREP" else ("DY", "AY")
        x = 0
        for (who, q, e) in pieces:
            a, b = 512 * q, 512 * e
            lst = ind(win, R(off, 32 * q, 32 * e))
            if who == "S":
                P, raw = R(("p2", "p5")[x], 0, 512), R("GR", 512 * x, 512 * x + 512)
                x = 1 - x
                act(raw, lst, ACT.Copy)
                mm(zsub(P, t, q) if sub == "ZREP" else (P, NIDB, R(sub, a + sh, b + sh), True, False))
                mm((P, IDB, raw, False, True))
                act(R(AG, a, b), P, ACT.Abs)
            else:
                tt(R(DG, a, b), lst, R(sub, a + sh, b + sh), ALU.subtract)
                if who == "V": act(R(AG, a, b), R(DG, a, b), ACT.Abs)
                else: ts(R(AG, a, b), R(DG, a, b), 0.0, ALU.max)

    def lanesum(out, buf, a, b, ks, w):
        mm(*[(R(out[0], out[1] + k, out[1] + 128, 16, 32 * a, 32 * b), R(buf, 512 * a + k, 512 * b, 16), WEIGHT[w], False, False) for k in range(ks)])

    def sums(out, x, t, ks, w):
        for (what, a, b) in plan(x + "S", t):
            lanesum(out, ("D" if what == "D" else "A") + x, a, b, ks, {"A": w, "P": 2 * w, "D": -w}[what])

    def gstage(t):
        mm((KEY, ONES, F("CRI"), True, False))
        dist(WG, "EU", "ZREP", 0, plan("G", t), t)
        sums(KEY, "G", t, 16, 32768)
        mm((KEY, F("EH"), IDB, False, True))

    def argstage(t):
        scan(F("KMIN"), F("RS"), KEY, ALU.max, ALU.min)
        ts(F("KA"), END("KMIN"), 2047, ALU.bitwise_and)
        tt(F("ERM"), ind(F("KA"), REP), F("M16"), ALU.mult)
        mm((E8, IDB, G8(5), True, False), (E8, F("ERM"), C8, False, True))
        ts(F("E8U"), E8, -128.0, ALU.add)
        cp(F("JU"), ind(F("IXI") if t == 0 else WI, F("E8U")))
        (cast if CFG["JH"][t] == "G" else cp)(F("JH%d" % (t & 1)), F("JU"))

    def lkx(t):
        lk = F("LKI") if t == 0 else WL
        for (_, a, b) in plan("L", t):
            tt(R("LG", 512 * a, 512 * b), ind(lk, R("JU", 32 * a, 32 * b)), R("MK", 0, 512 * (b - a)), ALU.mult)
        for h in (0, 1):
            p = R(("p3", "p4")[h], 0, 64)
            mm(*[(p, IDB, R("LG", 1024 * h + k, 1024 * h + 1024, 16), k == 0, k == 15) for k in range(16)])
            cp(R("NU", 64 * h, 64 * h + 64), p)
        for (w, a, b) in plan("X", t):
            o, lst = R("XG", 512 * a, 512 * b), ind(WX, R("JU", 32 * a, 32 * b))
            if w == "S": act(o, lst, ACT.Copy)
            else: cp(o, lst)

    def pairs(masked, plain, bank, who, x):
        seg = lambda c: R("p6", SEG[c], SEG[c] + 16 * c + 16) if SEG[c] < 432 else R(bank, SEG[c] - 224, SEG[c] - 208 + 16 * c)
        for (a, b, P) in ((0, 432, R("p6", 0, 432)), (432, 576, R(bank, 208, 352))):
            cs = [c for c in range(8) if a <= SEG[c] < b]
            mm((P, F(masked), R("R2", a, b), True, False), *[(seg(c), F(plain), R("P4K", 0, 16 * c + 16), False, c == cs[-1]) for c in cs])
            if who == "S": act(R("XA", a, b), P, ACT.Abs)
        if who == "S":
            scan(F("XS"), F("RD"), F("XA"), ALU.max, ALU.min)
            tt(R("TW", x, x + 16), ind(F("XS"), C("ENDS")), F("DUMP"), ALU.add)
        else:
            for c in range(8):
                least(C("TW", x + 8 + c), seg(c))
            tt(R("TW", x, x + 8), R("TW", x + 8, x + 16), D8("DUMP"), ALU.add)
        return R("TW", x, x + 8)

    def idx(t):
        if CFG["EI"][t] == "V": cp(F("ERU"), ind(F("KA"), REP))
        else:
            cast(S8(7), F("KA"))
            act(F("ERF"), ind(S8(7), REP), ACT.Copy)
            cast(F("ERU"), F("ERF"))
        w = pairs("ERM", "ERU", "p1", CFG["WI"][t], 0)
        tt(F("NOFF"), E8, w, ALU.min)

    def znext(t):
        for (_, a, b) in plan("M", t):
            scan(R("XM", 512 * a, 512 * b), R("RX", 0, 512 * (b - a)), R("XG", 512 * a, 512 * b), ALU.mult, ALU.max)
        mm((PU, F("HID"), F("Z%d" % t), True, False), (PU, F("HID"), R("XM", 15, 2048, 16), False, True))
        if CFG["ZN"][t] == "V": ts(F("ZN%d" % t), PU, 12582912.0, ALU.add, -12582912.0, ALU.add)
        else:
            act(F("ZH"), PU, ACT.Copy, bias=130.0)
            act(F("ZN%d" % t), F("ZH"), ACT.Copy, bias=-130.0)
        if t < RO - 1:
            m["send"](F("Z%d" % (t + 1)), F("ZN%d" % t), "za%d" % (t + 1), T.cores[(rank + 1) % n], core, topo)
        else:
            m["send"](F("ZR"), F("ZN%d" % t), "zr", T.cores[(rank - t) % n], core, topo)

    def far(t):
        P = R("p7", 0, 512)
        for q in range(4):
            a, b = 512 * q, 512 * q + 512
            mm(zsub(P, t, q), (P, IDB, R("XG", a, b), False, True))
            act(R("AF", a, b), P, ACT.Abs)

    def ystage(t):
        mm((PZ, ONES, F("CRL"), True, False))
        dist(WX, "NU", "XG", 1, plan("Y", t))
        sums(PZ, "Y", t, 15, -32768)
        mm((PZ, F("JH%d" % (t & 1)), IDB, False, True))

    def rec(t):
        tt(F("CMP"), PZ, F("THR"), ALU.is_ge)
        scan(F("KMX"), F("RS"), PZ, ALU.max, ALU.min)
        scan(F("CNS"), F("RC"), F("CMP"), ALU.min, ALU.add)
        act(F("RS8"), END("CNS"), ACT.Sign, acc=F("ACC") if t < RO - 1 else None)
        tt(F("NRM"), ind(F("CNS"), LAST), F("TH16"), ALU.is_lt)

    def gists(t):
        mm((GD8, IDB, G8(7), True, False), (GD8, F("NRM"), F("DL"), False, True))
        tt(F("GOFF"), GD8, F("NOFF"), ALU.min)
        cp(ind(F("GI"), F("GOFF")), F("Z%d" % t))

    def names(t):
        mm((FT, ONES, F("TB"), True, False))
        lanesum(FT, "AF", 0, 4, 16, 1)
        mm(*[(R("p4", 128 + k, 256, 16), P4K, F("RS8"), False, k == 15) for k in range(16)])
        act(F("SG"), FT, ACT.Sign, bias=4095.5)
        a, b = R("p4", 256, 384), R("p4", 384, 512)
        mm((a, IDB, F("VH%d" % (t & 1)), True, False), (a, F("SG"), P4K, False, True), (b, IDB, F("JH%d" % (t & 1)), True, False), (b, F("SG"), N4K, False, True))
        act(F("NA"), PNA, ACT.Copy, bias=-4096.0)
        tt(ind(F("IX"), F("NOFF")), R("NA", 0, 128), R("NA", 128, 256), ALU.max)

    def links(t):
        ts(F("KJ"), END("KMX"), 2047, ALU.bitwise_and)
        if CFG["RF"][t] == "S": act(S8(2), F("RS8"), ACT.Copy, scale=-2048.5, bias=-2047.5)
        else: ts(S8(2), END("CNS"), -8192.0, ALU.mult, 1.0, ALU.min)
        PLA, PLB = [R(b, x, x + 128) for b, x in CFG["LB"][t]]
        tt(S8(3), F("KJ"), S8(2), ALU.add)
        tt(F("ERM2"), ind(S8(3), REP), F("NRM"), ALU.mult)
        if CFG["EL"][t] == "V": ts(F("ERU2"), ind(S8(3), REP), 0.0, ALU.max)
        else:
            act(F("ERF2"), ind(S8(3), REP), ACT.Relu)
            cast(F("ERU2"), F("ERF2"))
        cast(F("KE"), END("KMX"))
        tt(R("STEP", 16, 144), ind(R("KE", 0, 8), REP), F("KMX"), ALU.is_equal)
        now, was = R("STEP", 16, 144), R("STEP", 15, 143)
        mm((J8, IDB, G8(6), True, False), (J8, F("ERM2"), C8, False, True))
        ts(F("JX8"), J8, -128.0, ALU.add)
        w = pairs("ERM2", "ERU2", "p3", CFG["WL"][t], 16)
        tt(F("LOFF"), J8, w, ALU.min)
        mm((PLB, SHB, F("JH%d" % (t & 1)), True, False), (PLB, now, P4K, False, False), (PLB, was, N4K, False, True))
        act(R("LA", 128, 256), PLB, ACT.Identity, bias=C("BB"))
        if CFG["TO"][t] == "V":
            mm((PLA, now, N4K, True, False), (PLA, was, P4K, False, True))
            act(R("LA", 0, 128), PLA, ACT.Identity, bias=C("BA"))
            tt(F("TOLD"), ind(WL, F("JX8")), R("LA", 0, 128), ALU.add)
        else:
            act(R("LA", 0, 128), ind(WL, F("JX8")), ACT.Copy)
            mm((PLA, now, N4K, True, False), (PLA, was, P4K, False, False), (PLA, F("IDF"), R("LA", 0, 128), False, True))
            act(F("TOLD"), PLA, ACT.Identity, bias=C("BA"))
        tt(ind(F("LK"), F("LOFF")), F("TOLD"), R("LA", 128, 256), ALU.max)

    ustage(0)
    for t in range(RO):
        gstage(t)
        argstage(t)
        lkx(t)
        if t == 0:
            for h in range(0, 2048, 512):
                cast(R("LK", h + 128, h + 640), R("LKI", h, h + 512))
        idx(t)
        znext(t)
        ystage(t)
        rec(t)
        if t < RO - 1:
            gists(t)
            ustage(t + 1)
            estage(t + 1)
        far(t)
        names(t)
        links(t)
    dma("S", "yi", WI)
    dma("Y", "yl", WL)
    dma("Y", "yz", F("ZR"))
    m["run"]()
